import numpy as np
import ml_dtypes


def mxq(x, axis, fmt="e4m3"):
    dtype, down = {"e4m3": (ml_dtypes.float8_e4m3fn, 7), "e5m2": (ml_dtypes.float8_e5m2, 14)}[fmt]
    v = np.moveaxis(np.asarray(x, np.float32).astype(ml_dtypes.bfloat16).astype(np.float64), axis, -1)
    blocks = v.reshape(v.shape[:-1] + (-1, 32))
    amax = np.abs(blocks).max(-1, keepdims=True)
    byte = np.maximum(np.where(amax > 0, np.frexp(amax)[1] - 1 + 127, 0) - down, 1)
    scale = np.exp2(byte - 127.0)
    codes = (blocks / scale).astype(np.float32).astype(dtype).astype(np.float64)
    return np.moveaxis((codes * scale).reshape(v.shape), -1, axis)


WIDE = False


def mx_kscale(k):
    if not WIDE:
        return np.ones(k)
    levels = np.array([10, -10, 5, -5, 0])
    if k % 512:
        return np.exp2(np.random.permutation(np.resize(levels, k // 32))).repeat(32)
    a = np.empty((k // 512, 16))
    for p in range(k // 512):
        a[p, :8] = np.random.permutation(np.resize(levels, 8))
        for g in range(8):
            far = levels[np.abs(levels - a[p, g]) >= 10]
            a[p, g + 8] = far[np.random.randint(len(far))]
    return np.exp2(a.ravel()).repeat(32)


BF16 = ml_dtypes.bfloat16


def bf(x):
    return np.asarray(x, np.float32).astype(BF16)


def f64(x):
    return np.asarray(x).astype(np.float64)

def planes(Y):
    n, m = Y.shape
    b = f64(bf(Y)).reshape(n // 32, 32, m)
    amax = np.abs(b).max(1)
    byte = np.clip(np.where(amax > 0, np.frexp(amax)[1] - 1 + 127 - 7, 1), 1, 254)
    codes = (b * np.exp2(127.0 - byte)[:, None, :]).reshape(n, m).astype(np.float32).astype(ml_dtypes.float8_e4m3fn).view(np.uint8)
    words = codes.reshape(n // 512, 128, 4, m).transpose(0, 1, 3, 2)
    return np.ascontiguousarray(words), np.ascontiguousarray(byte.astype(np.uint8).reshape(n // 512, 16, m))


T, I, D, N = 1024, 2048, 1024, 1536
FMT = "e4m3"

def setup_inputs():
    s_item = mx_kscale(I)
    s_ctx = mx_kscale(D)
    spread = np.exp(0.8 * np.random.randn(N))
    history = np.random.randn(T, I) * s_item[None, :]
    item_factors = np.random.randn(I, N) / np.sqrt(I) * spread[None, :] / s_item[:, None]
    context = np.random.randn(T, D) * s_ctx[None, :]
    w_context = 1.5 * np.random.randn(D, N) / np.sqrt(D) / s_ctx[:, None]
    b_context = 0.5 * np.random.randn(N)
    user_factors = np.random.randn(T, N) * spread[None, :]
    return {"history": bf(history), "item_factors": bf(item_factors),
            "context": bf(context), "w_context": bf(w_context),
            "b_context": bf(b_context), "user_factors": bf(user_factors)}

def reference(history, item_factors, context, w_context, b_context, user_factors):
    implicit = mxq(f64(history), 1, FMT) @ mxq(f64(item_factors), 0, FMT)
    logits = mxq(f64(context), 1, FMT) @ mxq(f64(w_context), 0, FMT)
    gate = 1.0 / (1.0 + np.exp(-(logits + f64(b_context))))
    y = (f64(user_factors) + implicit) * gate
    Y = y.T
    words, scales = planes(Y)
    return y, words, scales

@@ -1,0 +1,353 @@
+from contextlib import ExitStack
+
+import concourse.mybir as mybir
+from concourse.masks import make_identity
+
+T, I, D, N = 1024, 2048, 1024, 1536
+FLOPS = 2 * T * (I + D) * N
+
+F32 = mybir.dt.float32
+BF16 = mybir.dt.bfloat16
+U32 = mybir.dt.uint32
+I32 = mybir.dt.int32
+U8 = mybir.dt.uint8
+FP8X4 = mybir.dt.float8_e4m3fn_x4
+ADD = mybir.AluOpType.add
+MULT = mybir.AluOpType.mult
+SIGMOID = mybir.ActivationFunctionType.Sigmoid
+
+P = 128
+PACK = 4
+K_PASS = P * PACK
+NG = 512
+HALF = NG // 2
+GROUPS = N // NG
+TILES = T // P
+STEPS = GROUPS * TILES
+CTX_PASSES = D // K_PASS
+PASSES = (D + I) // K_PASS
+CHUNKS = PASSES // 2
+AHEAD = 2
+HEAD_SHARE = 144
+SHARES = (144, 160, 96)
+HALVES = (0, 1, 2, 2, 2, 2, 3, 0, 2, 2, 2, 2, 2, 1, 1, 0)
+STORE_LAG = 4
+W_LEAD = 2
+
+
+def tile_svdpp_context_gate_g1_kernel(
+    tc, history, item_factors, context, w_context, b_context, user_factors, out_0, out_1, out_2
+):
+    nc = tc.nc
+    with ExitStack() as ctx:
+        keep = ctx.enter_context(tc.tile_pool(name="keep", bufs=1))
+        ring = ctx.enter_context(tc.tile_pool(name="ring", bufs=2))
+        psum = ctx.enter_context(tc.psum_pool(name="psum", bufs=2))
+        ctx.enter_context(tc.manual_schedule())
+
+        tiles = {}
+
+        ident = keep.tile([P, P], F32, name="ident")
+        make_identity(nc, ident[:])
+
+        def load_bias():
+            b_rows = keep.tile([P, GROUPS, PACK], BF16, name="b_rows")
+            nc.sync.dma_start(out=b_rows[:], in_=b_context.rearrange("(j p c) -> p j c", p=P, c=PACK))
+            tiles["b_rows"] = b_rows
+
+        def widen_bias():
+            b_wide = keep.tile([P, GROUPS, PACK], F32, name="b_wide")
+            nc.vector.tensor_copy(out=b_wide[:], in_=tiles["b_rows"][:])
+            tiles["b_wide"] = b_wide
+
+        def spread_bias(j):
+            bank = psum.tile([P, PACK, P], F32, name="turn", bufs=4)
+            for c in range(PACK):
+                nc.tensor.transpose(bank[:, c, :], tiles["b_wide"][:, j, c : c + 1].to_broadcast([P, P]), ident[:])
+            bias = keep.tile([P, NG], F32, name="bias%d" % j)
+            nc.scalar.copy(out=bias[:].rearrange("m (p c) -> m p c", c=PACK), in_=bank[:].rearrange("m c p -> m p c"))
+            tiles["bias", j] = bias
+
+        def warm_sigmoid():
+            warm = keep.tile([P, 1], F32, name="warm")
+            nc.scalar.activation(out=warm[:], in_=ident[:, 0:1], func=SIGMOID)
+
+        def load_context(i):
+            raw = ring.tile([P, D], BF16, name="ctx_raw", bufs=4)
+            nc.sync.dma_start(out=raw[:], in_=context[i * P : (i + 1) * P, :])
+            tiles["ctx_raw", i] = raw
+
+        def load_history(i):
+            raw = ring.tile([P, I], BF16, name="hist_raw", bufs=4)
+            nc.sync.dma_start(out=raw[:], in_=history[i * P : (i + 1) * P, :])
+            tiles["hist_raw", i] = raw
+
+        def load_weight(j, g):
+            src = w_context if g < CTX_PASSES else item_factors
+            k0 = (g if g < CTX_PASSES else g - CTX_PASSES) * K_PASS
+            raw = ring.tile([P, PACK, NG], BF16, name="w_raw", bufs=8)
+            nc.sync.dma_start(
+                out=raw[:],
+                in_=src[k0 : k0 + K_PASS, j * NG : (j + 1) * NG].rearrange("(p t) n -> p t n", t=PACK),
+            )
+            tiles["w_raw", j, g] = raw
+
+        def load_user(j, half):
+            rows = TILES // 2
+            raw = ring.tile([P, rows, NG], BF16, name="user", bufs=3)
+            nc.sync.dma_start(
+                out=raw[:],
+                in_=user_factors[half * rows * P : (half + 1) * rows * P, j * NG : (j + 1) * NG].rearrange(
+                    "(i p) n -> p i n", p=P
+                ),
+            )
+            tiles["user", j, half] = raw
+
+        def turn_activations(i, c):
+            if c == 0:
+                words = tiles["ctx_raw", i][:].bitcast(F32)
+            else:
+                words = tiles["hist_raw", i][:, (c - 1) * 2 * K_PASS : c * 2 * K_PASS].bitcast(F32)
+            bank = psum.tile([P, 2, 2, P], F32, name="turn", bufs=4)
+            for g in range(2):
+                for u in range(2):
+                    nc.tensor.transpose(bank[:, g, u, :], words[:, 2 * P * g + u : 2 * P * (g + 1) : 2], ident[:])
+            tiles["act_bank", i, c] = bank
+
+        def drain_activations(i, c):
+            grouped = ring.tile([P, 2 * K_PASS], BF16, name="act_grouped", bufs=4, align_bytes=64)
+            nc.scalar.copy(
+                out=grouped[:].bitcast(F32).rearrange("p (g r u) -> p g r u", g=2, u=2),
+                in_=tiles["act_bank", i, c][:].rearrange("p g u r -> p g r u"),
+            )
+            tiles["act_grouped", i, c] = grouped
+
+        def quantize_activations(i, c):
+            codes = keep.tile([P, 2 * P], U32, name="act_codes%d_%d" % (i, c), align_bytes=64)
+            scales = keep.tile([P, 2 * P], U8, name="act_scales%d_%d" % (i, c), align_bytes=64)
+            nc.vector.quantize_mx(out=codes[:].bitcast(FP8X4), scales=scales[:], in_=tiles["act_grouped", i, c][:])
+            tiles["act_mx", i, c] = (codes, scales)
+
+        def interleave(copy, j, h, c0, c1):
+            g, half = divmod(h, 2)
+            if ("w_grouped", j, h) not in tiles:
+                tiles["w_grouped", j, h] = ring.tile([P, HALF, PACK], BF16, name="w_grouped", bufs=6, align_bytes=64)
+            src = tiles["w_raw", j, g][:, :, half * HALF + c0 : half * HALF + c1]
+            copy(
+                out=tiles["w_grouped", j, h][:, c0:c1, :].rearrange("p (c i) t -> p c t i", i=4),
+                in_=src.rearrange("p t (c i) -> p c t i", i=4),
+            )
+
+        def interleave_vector(j, h, share):
+            interleave(nc.vector.tensor_copy, j, h, 0, share)
+
+        def interleave_scalar(j, h, share):
+            interleave(nc.scalar.copy, j, h, share, HALF)
+
+        def quantize_weight(j, h):
+            g, half = divmod(h, 2)
+            if half == 0:
+                codes = ring.tile([P, NG], U32, name="w_codes", bufs=2 * PASSES, align_bytes=64)
+                scales = ring.tile([P, NG], U8, name="w_scales", bufs=2 * PASSES, align_bytes=64)
+                tiles["w_mx", j, g] = (codes, scales)
+            codes, scales = tiles["w_mx", j, g]
+            cols = slice(half * HALF, (half + 1) * HALF)
+            nc.vector.quantize_mx(
+                out=codes[:, cols].bitcast(FP8X4),
+                scales=scales[:, cols],
+                in_=tiles["w_grouped", j, h][:].rearrange("p n t -> p (n t)"),
+            )
+
+        def multiply(s, name, g0, g1):
+            j, i = divmod(s, TILES)
+            bank = psum.tile([P, NG], F32, name=name)
+            for g in range(g0, g1):
+                a_codes, a_scales = tiles["act_mx", i, g // 2]
+                w_codes, w_scales = tiles["w_mx", j, g]
+                cols = slice((g % 2) * P, (g % 2 + 1) * P)
+                nc.tensor.matmul_mx(
+                    out=bank[:],
+                    lhsT=a_codes[:, cols].bitcast(FP8X4),
+                    lhsT_scale=a_scales[:, cols],
+                    rhs=w_codes[:].bitcast(FP8X4),
+                    rhs_scale=w_scales[:],
+                    start=(g == g0),
+                    stop=(g == g1 - 1),
+                )
+            tiles[name, s] = bank
+
+        def add_bias(s):
+            z = ring.tile([P, NG], F32, name="z")
+            nc.vector.tensor_tensor(out=z[:], in0=tiles["logits", s][:], in1=tiles["bias", s // TILES][:], op=ADD)
+            tiles["z", s] = z
+
+        def sigmoid(s):
+            gate = ring.tile([P, NG], F32, name="gate", bufs=3)
+            nc.scalar.activation(out=gate[:], in_=tiles["z", s][:], func=SIGMOID)
+            tiles["gate", s] = gate
+
+        def add_user(s):
+            j, i = divmod(s, TILES)
+            half, row = divmod(i, TILES // 2)
+            total = ring.tile([P, NG], F32, name="total", bufs=3)
+            nc.vector.tensor_tensor(
+                out=total[:], in0=tiles["implicit", s][:], in1=tiles["user", j, half][:, row, :], op=ADD
+            )
+            tiles["total", s] = total
+
+        def apply_gate(s):
+            y = ring.tile([P, NG], F32, name="y", bufs=STORE_LAG + 2)
+            nc.vector.tensor_tensor(out=y[:], in0=tiles["total", s][:], in1=tiles["gate", s][:], op=MULT)
+            tiles["y", s] = y
+
+        def round_y(s):
+            y_bf = ring.tile([P, NG], BF16, name="y_bf", bufs=4)
+            nc.scalar.copy(
+                out=y_bf[:].rearrange("m (u p e) -> m u p e", u=2, e=2),
+                in_=tiles["y", s][:].rearrange("m (p u e) -> m u p e", u=2, e=2),
+            )
+            tiles["y_bf", s] = y_bf
+
+        def turn_y(pair):
+            bank = psum.tile([P, 2, 2, P], F32, name="turn", bufs=4)
+            for a in range(2):
+                words = tiles["y_bf", 2 * pair + a][:].bitcast(F32)
+                for u in range(2):
+                    nc.tensor.transpose(bank[:, a, u, :], words[:, u * P : (u + 1) * P], ident[:])
+            tiles["y_bank", pair] = bank
+
+        def drain_y(pair):
+            grouped = ring.tile([P, 2 * K_PASS], BF16, name="y_grouped", align_bytes=64)
+            nc.scalar.copy(
+                out=grouped[:].bitcast(F32).rearrange("p (a r u) -> p a r u", a=2, u=2),
+                in_=tiles["y_bank", pair][:].rearrange("p a u r -> p a r u"),
+            )
+            tiles["y_grouped", pair] = grouped
+
+        def quantize_y(pair):
+            j, q = divmod(pair, TILES // 2)
+            if q == 0:
+                codes = ring.tile([P, T], U32, name="y_codes", align_bytes=64)
+                scales = ring.tile([P, T], U8, name="y_scales", align_bytes=64)
+                tiles["y_mx", j] = (codes, scales)
+            codes, scales = tiles["y_mx", j]
+            cols = slice(q * 2 * P, (q + 1) * 2 * P)
+            nc.vector.quantize_mx(
+                out=codes[:, cols].bitcast(FP8X4), scales=scales[:, cols], in_=tiles["y_grouped", pair][:]
+            )
+
+        def store_y(s):
+            j, i = divmod(s, TILES)
+            nc.sync.dma_start(out=out_0[i * P : (i + 1) * P, j * NG : (j + 1) * NG], in_=tiles["y", s][:])
+
+        def store_codes(j, half):
+            cols = slice(half * T // 2, (half + 1) * T // 2)
+            words = out_1[j].rearrange("p m t -> p (m t)").bitcast(I32)
+            nc.sync.dma_start(out=words[:, cols], in_=tiles["y_mx", j][0][:, cols].bitcast(I32))
+
+        def store_scales(j):
+            scales = tiles["y_mx", j][1]
+            for q in range(4):
+                nc.sync.dma_start(
+                    out=out_2[j, 4 * q : 4 * q + 4, :].bitcast(I32), in_=scales[32 * q : 32 * q + 4, :].bitcast(I32)
+                )
+
+        load_bias()
+        load_context(0)
+        load_weight(0, 0)
+        load_history(0)
+        load_weight(0, 1)
+        load_weight(0, 2)
+        load_weight(0, 3)
+        load_context(1)
+        load_history(1)
+        load_weight(0, 4)
+        load_weight(0, 5)
+        load_context(2)
+        load_history(2)
+        load_user(0, 0)
+        load_weight(1, 0)
+        load_context(3)
+        load_history(3)
+        warm_sigmoid()
+        widen_bias()
+        spread_bias(0)
+        for c in range(CHUNKS):
+            turn_activations(0, c)
+        for g in range(PASSES):
+            if g < CHUNKS:
+                drain_activations(0, g)
+            for half in range(2):
+                h = 2 * g + half
+                interleave_vector(0, h, HEAD_SHARE)
+                interleave_scalar(0, h, HEAD_SHARE)
+                if h >= 1:
+                    quantize_weight(0, h - 1)
+            if g < CHUNKS:
+                quantize_activations(0, g)
+        quantize_weight(0, 2 * PASSES - 1)
+        for c in range(CHUNKS):
+            turn_activations(1, c)
+
+        done = 0
+        loaded = 1
+        halves = []
+        for s in range(STEPS + 8):
+            j, i = divmod(s, TILES)
+            count = HALVES[s] if s < len(HALVES) else 0
+            previous = halves
+            halves = [divmod(h, 2 * PASSES) for h in range(done, done + count)]
+            done = done + count
+            share = SHARES[0 if s + 1 < TILES - 1 else 1 + j] if count else 0
+
+            if s + 1 < TILES:
+                for c in range(CHUNKS):
+                    drain_activations(s + 1, c)
+            if s % 2 == 0 and 0 <= (s - 6) // 2 < STEPS // 2:
+                drain_y((s - 6) // 2)
+
+            if s < STEPS:
+                multiply(s, "logits", 0, CTX_PASSES)
+                multiply(s, "implicit", CTX_PASSES, PASSES)
+            if s % 2 == 1 and 0 <= (s - 5) // 2 < STEPS // 2:
+                turn_y((s - 5) // 2)
+            if i == TILES - 2 and j + 1 < GROUPS:
+                spread_bias(j + 1)
+            if s + 2 < TILES:
+                for c in range(CHUNKS):
+                    turn_activations(s + 2, c)
+
+            if s + 4 < TILES:
+                load_context(s + 4)
+                load_history(s + 4)
+            if i in (1, 5) and s + 3 < STEPS:
+                load_user(*divmod((s + 3) // 4, 2))
+            while loaded < 2 * PASSES and loaded < done // 2 + W_LEAD:
+                load_weight(1 + loaded // PASSES, loaded % PASSES)
+                loaded = loaded + 1
+            if 0 <= s - STORE_LAG < STEPS:
+                store_y(s - STORE_LAG)
+            if s % 4 == 1 and 0 <= (s - 9) // 4 < 2 * GROUPS:
+                store_codes(*divmod((s - 9) // 4, 2))
+                if (s - 9) // 4 % 2 == 1:
+                    store_scales((s - 9) // 8)
+
+            if 0 <= s - 1 < STEPS:
+                add_bias(s - 1)
+            if 0 <= s - 3 < STEPS:
+                round_y(s - 3)
+            if 0 <= s - 2 < STEPS:
+                apply_gate(s - 2)
+            if 0 <= s - 1 < STEPS:
+                add_user(s - 1)
+                sigmoid(s - 1)
+            for jj, h in previous:
+                quantize_weight(jj + 1, h)
+            if s + 1 < TILES:
+                for c in range(CHUNKS):
+                    quantize_activations(s + 1, c)
+            if s % 2 == 0 and 0 <= (s - 6) // 2 < STEPS // 2:
+                quantize_y((s - 6) // 2)
+            for jj, h in halves:
+                interleave_vector(jj + 1, h, share)
+                interleave_scalar(jj + 1, h, share)

@@ -27,10 +27,15 @@ STEPS = GROUPS * TILES
 CTX_PASSES = D // K_PASS
 PASSES = (D + I) // K_PASS
 CHUNKS = PASSES // 2
-AHEAD = 2
 HEAD_SHARE = 144
-SHARES = (144, 160, 96)
-HALVES = (0, 1, 2, 2, 2, 2, 3, 0, 2, 2, 2, 2, 2, 1, 1, 0)
+SHARES = (288, 288)
+UNITS = (0, 1, 1, 1, 1, 1, 1, 0, 1, 1, 1, 1, 1, 0, 1, 0)
+TURNED = (1,)
+HEAD_LOADS = "w00 w01 c0 w02 h0 w03 c1 w04 h1 w05 h2 u c2 h3 w10"
+HEAD_JOBS = ("", "b", "c0", "h0 l", "c1", "")
+LEAD = 1
+C3 = 0
+ROUND = ("scalar", "scalar", "scalar")
 STORE_LAG = 4
 W_LEAD = 2
 
@@ -51,31 +56,42 @@ def tile_svdpp_context_gate_g1_kernel(
         make_identity(nc, ident[:])
 
         def load_bias():
-            b_rows = keep.tile([P, GROUPS, PACK], BF16, name="b_rows")
-            nc.sync.dma_start(out=b_rows[:], in_=b_context.rearrange("(j p c) -> p j c", p=P, c=PACK))
+            b_rows = keep.tile([N // P, P], BF16, name="b_rows")
+            nc.scalar.dma_start(out=b_rows[:], in_=b_context.rearrange("(c p) -> c p", p=P))
             tiles["b_rows"] = b_rows
 
-        def widen_bias():
-            b_wide = keep.tile([P, GROUPS, PACK], F32, name="b_wide")
-            nc.vector.tensor_copy(out=b_wide[:], in_=tiles["b_rows"][:])
-            tiles["b_wide"] = b_wide
+        def turn_bias():
+            b_wide = keep.tile([P, P], F32, name="b_wide")
+            nc.gpsimd.memset(b_wide[:], 0.0)
+            nc.vector.tensor_copy(out=b_wide[0 : N // P, :], in_=tiles["b_rows"][:])
+            bank = psum.tile([P, P], F32, name="turn", bufs=4)
+            nc.tensor.transpose(bank[:], b_wide[:], ident[:])
+            b_cols = keep.tile([P, N // P], F32, name="b_cols")
+            nc.vector.tensor_copy(out=b_cols[:], in_=bank[:, 0 : N // P])
+            tiles["b_cols"] = b_cols
 
         def spread_bias(j):
-            bank = psum.tile([P, PACK, P], F32, name="turn", bufs=4)
+            bank = psum.tile([P, NG], F32, name="turn", bufs=4)
             for c in range(PACK):
-                nc.tensor.transpose(bank[:, c, :], tiles["b_wide"][:, j, c : c + 1].to_broadcast([P, P]), ident[:])
+                col = PACK * j + c
+                nc.tensor.transpose(
+                    bank[:, c * P : (c + 1) * P], tiles["b_cols"][:, col : col + 1].to_broadcast([P, P]), ident[:]
+                )
+            tiles["bias_bank", j] = bank
+
+        def drain_bias(j):
             bias = keep.tile([P, NG], F32, name="bias%d" % j)
-            nc.scalar.copy(out=bias[:].rearrange("m (p c) -> m p c", c=PACK), in_=bank[:].rearrange("m c p -> m p c"))
+            nc.scalar.copy(out=bias[:], in_=tiles["bias_bank", j][:])
             tiles["bias", j] = bias
 
         def warm_sigmoid():
             warm = keep.tile([P, 1], F32, name="warm")
             nc.scalar.activation(out=warm[:], in_=ident[:, 0:1], func=SIGMOID)
 
-        def load_context(i):
-            raw = ring.tile([P, D], BF16, name="ctx_raw", bufs=4)
-            nc.sync.dma_start(out=raw[:], in_=context[i * P : (i + 1) * P, :])
-            tiles["ctx_raw", i] = raw
+        def load_context(q):
+            raw = ring.tile([P, 2, D], BF16, name="ctx_raw", bufs=3)
+            nc.sync.dma_start(out=raw[:], in_=context[q * 2 * P : (q + 1) * 2 * P, :].rearrange("(a p) k -> p a k", p=P))
+            tiles["ctx_raw", q] = raw
 
         def load_history(i):
             raw = ring.tile([P, I], BF16, name="hist_raw", bufs=4)
@@ -92,89 +108,152 @@ def tile_svdpp_context_gate_g1_kernel(
             )
             tiles["w_raw", j, g] = raw
 
-        def load_user(j, half):
-            rows = TILES // 2
-            raw = ring.tile([P, rows, NG], BF16, name="user", bufs=3)
+        def load_user(q):
+            j, i = divmod(2 * q, TILES)
+            raw = ring.tile([P, 2, NG], BF16, name="user", bufs=4)
             nc.sync.dma_start(
                 out=raw[:],
-                in_=user_factors[half * rows * P : (half + 1) * rows * P, j * NG : (j + 1) * NG].rearrange(
-                    "(i p) n -> p i n", p=P
-                ),
+                in_=user_factors[i * P : (i + 2) * P, j * NG : (j + 1) * NG].rearrange("(a p) n -> p a n", p=P),
             )
-            tiles["user", j, half] = raw
+            tiles["user", q] = raw
 
-        def turn_activations(i, c):
-            if c == 0:
-                words = tiles["ctx_raw", i][:].bitcast(F32)
-            else:
-                words = tiles["hist_raw", i][:, (c - 1) * 2 * K_PASS : c * 2 * K_PASS].bitcast(F32)
+        def turn_words(key, sources):
             bank = psum.tile([P, 2, 2, P], F32, name="turn", bufs=4)
-            for g in range(2):
+            for a in range(2):
                 for u in range(2):
-                    nc.tensor.transpose(bank[:, g, u, :], words[:, 2 * P * g + u : 2 * P * (g + 1) : 2], ident[:])
-            tiles["act_bank", i, c] = bank
+                    nc.tensor.transpose(bank[:, a, u, :], sources[a][:, u : 2 * P : 2], ident[:])
+            tiles[key] = bank
 
-        def drain_activations(i, c):
-            grouped = ring.tile([P, 2 * K_PASS], BF16, name="act_grouped", bufs=4, align_bytes=64)
+        def turn_context(c):
+            q, g = divmod(c, CTX_PASSES)
+            raw = tiles["ctx_raw", q]
+            turn_words(("ctx_bank", c), [raw[:, a, g * K_PASS : (g + 1) * K_PASS].bitcast(F32) for a in range(2)])
+
+        def turn_history(i, c):
+            raw = tiles["hist_raw", i]
+            passes = (2 * c, 2 * c + 1)
+            turn_words(("hist_bank", i, c), [raw[:, g * K_PASS : (g + 1) * K_PASS].bitcast(F32) for g in passes])
+
+        def drain(bank, grouped):
             nc.scalar.copy(
-                out=grouped[:].bitcast(F32).rearrange("p (g r u) -> p g r u", g=2, u=2),
-                in_=tiles["act_bank", i, c][:].rearrange("p g u r -> p g r u"),
+                out=grouped.bitcast(F32).rearrange("p (a r u) -> p a r u", a=2, u=2),
+                in_=bank[:].rearrange("p a u r -> p a r u"),
             )
-            tiles["act_grouped", i, c] = grouped
 
-        def quantize_activations(i, c):
-            codes = keep.tile([P, 2 * P], U32, name="act_codes%d_%d" % (i, c), align_bytes=64)
-            scales = keep.tile([P, 2 * P], U8, name="act_scales%d_%d" % (i, c), align_bytes=64)
-            nc.vector.quantize_mx(out=codes[:].bitcast(FP8X4), scales=scales[:], in_=tiles["act_grouped", i, c][:])
-            tiles["act_mx", i, c] = (codes, scales)
+        def drain_context(c):
+            grouped = ring.tile([P, 2 * K_PASS], BF16, name="ctx_grouped", bufs=3, align_bytes=64)
+            drain(tiles["ctx_bank", c], grouped[:])
+            tiles["ctx_grouped", c] = grouped
 
-        def interleave(copy, j, h, c0, c1):
-            g, half = divmod(h, 2)
-            if ("w_grouped", j, h) not in tiles:
-                tiles["w_grouped", j, h] = ring.tile([P, HALF, PACK], BF16, name="w_grouped", bufs=6, align_bytes=64)
-            src = tiles["w_raw", j, g][:, :, half * HALF + c0 : half * HALF + c1]
+        def drain_history(i, c):
+            if c == 0:
+                tiles["hist_grouped", i] = ring.tile([P, I], BF16, name="hist_grouped", bufs=2, align_bytes=64)
+            drain(tiles["hist_bank", i, c], tiles["hist_grouped", i][:, c * 2 * K_PASS : (c + 1) * 2 * K_PASS])
+
+        def quantize_context(c):
+            codes = keep.tile([P, 2 * P], U32, name="ctx_codes%d" % c, align_bytes=64)
+            scales = keep.tile([P, 2 * P], U8, name="ctx_scales%d" % c, align_bytes=64)
+            nc.vector.quantize_mx(out=codes[:].bitcast(FP8X4), scales=scales[:], in_=tiles["ctx_grouped", c][:])
+            tiles["ctx_mx", c] = (codes, scales)
+
+        def quantize_history(i):
+            codes = keep.tile([P, 4 * P], U32, name="hist_codes%d" % i, align_bytes=64)
+            scales = keep.tile([P, 4 * P], U8, name="hist_scales%d" % i, align_bytes=64)
+            nc.vector.quantize_mx(out=codes[:].bitcast(FP8X4), scales=scales[:], in_=tiles["hist_grouped", i][:])
+            tiles["hist_mx", i] = (codes, scales)
+
+        def interleave(copy, j, g, c0, c1):
+            if ("w_grouped", j, g) not in tiles:
+                tiles["w_grouped", j, g] = ring.tile([P, NG, PACK], BF16, name="w_grouped", bufs=3, align_bytes=64)
             copy(
-                out=tiles["w_grouped", j, h][:, c0:c1, :].rearrange("p (c i) t -> p c t i", i=4),
-                in_=src.rearrange("p t (c i) -> p c t i", i=4),
+                out=tiles["w_grouped", j, g][:, c0:c1, :].rearrange("p (c i) t -> p c t i", i=4),
+                in_=tiles["w_raw", j, g][:, :, c0:c1].rearrange("p t (c i) -> p c t i", i=4),
             )
 
-        def interleave_vector(j, h, share):
-            interleave(nc.vector.tensor_copy, j, h, 0, share)
+        def interleave_vector(j, g, c0, c1):
+            interleave(nc.vector.tensor_copy, j, g, c0, c1)
 
-        def interleave_scalar(j, h, share):
-            interleave(nc.scalar.copy, j, h, share, HALF)
+        def interleave_scalar(j, g, c0, c1):
+            interleave(nc.scalar.copy, j, g, c0, c1)
 
-        def quantize_weight(j, h):
-            g, half = divmod(h, 2)
-            if half == 0:
+        def quantize_weight(j, g, c0, c1):
+            if c0 == 0:
                 codes = ring.tile([P, NG], U32, name="w_codes", bufs=2 * PASSES, align_bytes=64)
                 scales = ring.tile([P, NG], U8, name="w_scales", bufs=2 * PASSES, align_bytes=64)
                 tiles["w_mx", j, g] = (codes, scales)
             codes, scales = tiles["w_mx", j, g]
-            cols = slice(half * HALF, (half + 1) * HALF)
             nc.vector.quantize_mx(
-                out=codes[:, cols].bitcast(FP8X4),
-                scales=scales[:, cols],
-                in_=tiles["w_grouped", j, h][:].rearrange("p n t -> p (n t)"),
+                out=codes[:, c0:c1].bitcast(FP8X4),
+                scales=scales[:, c0:c1],
+                in_=tiles["w_grouped", j, g][:, c0:c1, :].rearrange("p n t -> p (n t)"),
             )
 
-        def multiply(s, name, g0, g1):
-            j, i = divmod(s, TILES)
-            bank = psum.tile([P, NG], F32, name=name)
-            for g in range(g0, g1):
-                a_codes, a_scales = tiles["act_mx", i, g // 2]
-                w_codes, w_scales = tiles["w_mx", j, g]
-                cols = slice((g % 2) * P, (g % 2 + 1) * P)
+        def mx_group(out, passes):
+            for g, (stationary, s_cols, moving) in enumerate(passes):
                 nc.tensor.matmul_mx(
-                    out=bank[:],
-                    lhsT=a_codes[:, cols].bitcast(FP8X4),
-                    lhsT_scale=a_scales[:, cols],
-                    rhs=w_codes[:].bitcast(FP8X4),
-                    rhs_scale=w_scales[:],
-                    start=(g == g0),
-                    stop=(g == g1 - 1),
+                    out=out,
+                    lhsT=stationary[0][:, s_cols].bitcast(FP8X4),
+                    lhsT_scale=stationary[1][:, s_cols],
+                    rhs=moving[0][:].bitcast(FP8X4),
+                    rhs_scale=moving[1][:],
+                    start=(g == 0),
+                    stop=(g == len(passes) - 1),
                 )
-            tiles[name, s] = bank
+
+        def block(c):
+            return slice(c * P, (c + 1) * P)
+
+        def multiply_logits(s):
+            j, i = divmod(s, TILES)
+            bank = psum.tile([P, NG], F32, name="logits")
+            q, a = divmod(i, 2)
+            mx_group(
+                bank[:],
+                [(tiles["ctx_mx", CTX_PASSES * q + g], block(a), tiles["w_mx", j, g]) for g in range(CTX_PASSES)],
+            )
+            tiles["logits", s] = bank
+
+        def multiply_implicit(s):
+            j, i = divmod(s, TILES)
+            bank = psum.tile([P, NG], F32, name="implicit")
+            mx_group(
+                bank[:],
+                [(tiles["hist_mx", i], block(g), tiles["w_mx", j, CTX_PASSES + g]) for g in range(PASSES - CTX_PASSES)],
+            )
+            tiles["implicit", s] = bank
+
+        def multiply_logits_turned(s):
+            j, i = divmod(s, TILES)
+            q, b = divmod(i, 2)
+            bank = psum.tile([P, 2, 2 * P], F32, name="logits")
+            for c in range(2):
+                mx_group(
+                    bank[:, c, :],
+                    [
+                        (tiles["w_mx", j, g], block(2 * b + c), tiles["ctx_mx", CTX_PASSES * q + g])
+                        for g in range(CTX_PASSES)
+                    ],
+                )
+            tiles["logits_t", s] = bank
+
+        def sigmoid_turned(s):
+            j, b = s // TILES, s % 2
+            if b == 0:
+                tiles["gate_t", s // 2] = ring.tile([P, PACK, 2 * P], F32, name="gate_t")
+            for c in range(2):
+                col = PACK * j + 2 * b + c
+                nc.scalar.activation(
+                    out=tiles["gate_t", s // 2][:, 2 * b + c, :],
+                    in_=tiles["logits_t", s][:, c, :],
+                    func=SIGMOID,
+                    bias=tiles["b_cols"][:, col : col + 1],
+                )
+
+        def turn_gate(s):
+            bank = psum.tile([P, NG], F32, name="turn", bufs=4)
+            for c in range(PACK):
+                nc.tensor.transpose(bank[:, block(c)], tiles["gate_t", s // 2][:, c, block(s % 2)], ident[:])
+            tiles["gate", s] = bank
 
         def add_bias(s):
             z = ring.tile([P, NG], F32, name="z")
@@ -187,11 +266,9 @@ def tile_svdpp_context_gate_g1_kernel(
             tiles["gate", s] = gate
 
         def add_user(s):
-            j, i = divmod(s, TILES)
-            half, row = divmod(i, TILES // 2)
             total = ring.tile([P, NG], F32, name="total", bufs=3)
             nc.vector.tensor_tensor(
-                out=total[:], in0=tiles["implicit", s][:], in1=tiles["user", j, half][:, row, :], op=ADD
+                out=total[:], in0=tiles["implicit", s][:], in1=tiles["user", s // 2][:, s % 2, :], op=ADD
             )
             tiles["total", s] = total
 
@@ -200,154 +277,215 @@ def tile_svdpp_context_gate_g1_kernel(
             nc.vector.tensor_tensor(out=y[:], in0=tiles["total", s][:], in1=tiles["gate", s][:], op=MULT)
             tiles["y", s] = y
 
-        def round_y(s):
+        def round_y(s, engine):
             y_bf = ring.tile([P, NG], BF16, name="y_bf", bufs=4)
-            nc.scalar.copy(
-                out=y_bf[:].rearrange("m (u p e) -> m u p e", u=2, e=2),
-                in_=tiles["y", s][:].rearrange("m (p u e) -> m u p e", u=2, e=2),
-            )
+            dst = y_bf[:].rearrange("m (u p e) -> m u p e", u=2, e=2)
+            src = tiles["y", s][:].rearrange("m (p u e) -> m u p e", u=2, e=2)
+            if engine == "pool":
+                nc.gpsimd.tensor_scalar(out=dst, in0=src, scalar1=1.0, scalar2=0.0, op0=MULT, op1=ADD)
+            elif engine == "vector":
+                nc.vector.tensor_copy(out=dst, in_=src)
+            else:
+                nc.scalar.copy(out=dst, in_=src)
             tiles["y_bf", s] = y_bf
 
-        def turn_y(pair):
-            bank = psum.tile([P, 2, 2, P], F32, name="turn", bufs=4)
-            for a in range(2):
-                words = tiles["y_bf", 2 * pair + a][:].bitcast(F32)
+        def turn_y(s, count):
+            bank = psum.tile([P, count, 2, P], F32, name="turn", bufs=4)
+            for a in range(count):
+                words = tiles["y_bf", s + a][:].bitcast(F32)
                 for u in range(2):
-                    nc.tensor.transpose(bank[:, a, u, :], words[:, u * P : (u + 1) * P], ident[:])
-            tiles["y_bank", pair] = bank
+                    nc.tensor.transpose(bank[:, a, u, :], words[:, block(u)], ident[:])
+            tiles["y_bank", s] = bank
 
-        def drain_y(pair):
-            grouped = ring.tile([P, 2 * K_PASS], BF16, name="y_grouped", align_bytes=64)
+        def drain_y(s, count):
+            grouped = ring.tile([P, count * K_PASS], BF16, name="y_grouped", align_bytes=64)
             nc.scalar.copy(
-                out=grouped[:].bitcast(F32).rearrange("p (a r u) -> p a r u", a=2, u=2),
-                in_=tiles["y_bank", pair][:].rearrange("p a u r -> p a r u"),
+                out=grouped[:].bitcast(F32).rearrange("p (a r u) -> p a r u", a=count, u=2),
+                in_=tiles["y_bank", s][:].rearrange("p a u r -> p a r u"),
             )
-            tiles["y_grouped", pair] = grouped
+            tiles["y_grouped", s] = grouped
 
-        def quantize_y(pair):
-            j, q = divmod(pair, TILES // 2)
-            if q == 0:
+        def quantize_y(s, count):
+            j, i = divmod(s, TILES)
+            if i == 0:
                 codes = ring.tile([P, T], U32, name="y_codes", align_bytes=64)
                 scales = ring.tile([P, T], U8, name="y_scales", align_bytes=64)
                 tiles["y_mx", j] = (codes, scales)
             codes, scales = tiles["y_mx", j]
-            cols = slice(q * 2 * P, (q + 1) * 2 * P)
+            cols = slice(i * P, (i + count) * P)
             nc.vector.quantize_mx(
-                out=codes[:, cols].bitcast(FP8X4), scales=scales[:, cols], in_=tiles["y_grouped", pair][:]
+                out=codes[:, cols].bitcast(FP8X4), scales=scales[:, cols], in_=tiles["y_grouped", s][:]
             )
 
         def store_y(s):
             j, i = divmod(s, TILES)
             nc.sync.dma_start(out=out_0[i * P : (i + 1) * P, j * NG : (j + 1) * NG], in_=tiles["y", s][:])
 
-        def store_codes(j, half):
-            cols = slice(half * T // 2, (half + 1) * T // 2)
+        def store_codes(j, i0, i1):
+            cols = slice(i0 * P, i1 * P)
             words = out_1[j].rearrange("p m t -> p (m t)").bitcast(I32)
             nc.sync.dma_start(out=words[:, cols], in_=tiles["y_mx", j][0][:, cols].bitcast(I32))
 
-        def store_scales(j):
+        def store_scales(j, queues):
             scales = tiles["y_mx", j][1]
             for q in range(4):
-                nc.sync.dma_start(
+                queues[q % len(queues)].dma_start(
                     out=out_2[j, 4 * q : 4 * q + 4, :].bitcast(I32), in_=scales[32 * q : 32 * q + 4, :].bitcast(I32)
                 )
 
+        def turned(s):
+            return 0 <= s < STEPS and s // TILES in TURNED
+
+        def plain(s):
+            return 0 <= s < STEPS and s // TILES not in TURNED
+
         load_bias()
-        load_context(0)
-        load_weight(0, 0)
-        load_history(0)
-        load_weight(0, 1)
-        load_weight(0, 2)
-        load_weight(0, 3)
-        load_context(1)
-        load_history(1)
-        load_weight(0, 4)
-        load_weight(0, 5)
-        load_context(2)
-        load_history(2)
-        load_user(0, 0)
-        load_weight(1, 0)
-        load_context(3)
-        load_history(3)
+        for name in HEAD_LOADS.split():
+            if name[0] == "w":
+                load_weight(int(name[1]), int(name[2]))
+            elif name[0] == "c":
+                load_context(int(name[1]))
+            elif name[0] == "h":
+                load_history(int(name[1]))
+            else:
+                load_user(0)
         warm_sigmoid()
-        widen_bias()
-        spread_bias(0)
-        for c in range(CHUNKS):
-            turn_activations(0, c)
+        turn_bias()
         for g in range(PASSES):
-            if g < CHUNKS:
-                drain_activations(0, g)
+            jobs = HEAD_JOBS[g].split()
+            for name in jobs:
+                if name[0] == "c":
+                    for c in (2 * int(name[1]), 2 * int(name[1]) + 1):
+                        turn_context(c)
+                        drain_context(c)
+                elif name[0] == "h":
+                    for c in range(2):
+                        turn_history(int(name[1]), c)
+                        drain_history(int(name[1]), c)
+                elif name[0] == "l":
+                    multiply_logits(0)
+                else:
+                    spread_bias(0)
+                    drain_bias(0)
             for half in range(2):
-                h = 2 * g + half
-                interleave_vector(0, h, HEAD_SHARE)
-                interleave_scalar(0, h, HEAD_SHARE)
-                if h >= 1:
-                    quantize_weight(0, h - 1)
-            if g < CHUNKS:
-                quantize_activations(0, g)
-        quantize_weight(0, 2 * PASSES - 1)
-        for c in range(CHUNKS):
-            turn_activations(1, c)
+                c0 = half * HALF
+                interleave_vector(0, g, c0, c0 + HEAD_SHARE)
+                interleave_scalar(0, g, c0 + HEAD_SHARE, c0 + HALF)
+                if half == 1:
+                    quantize_weight(0, g, 0, HALF)
+                elif g >= 1:
+                    quantize_weight(0, g - 1, HALF, NG)
+            for name in jobs:
+                if name[0] == "c":
+                    quantize_context(2 * int(name[1]))
+                    quantize_context(2 * int(name[1]) + 1)
+                elif name[0] == "h":
+                    quantize_history(int(name[1]))
+        quantize_weight(0, PASSES - 1, HALF, NG)
+        turn_history(LEAD, 0)
+        turn_history(LEAD, 1)
 
         done = 0
         loaded = 1
-        halves = []
-        for s in range(STEPS + 8):
+        units = []
+        last = STEPS - 1
+        for s in range(STEPS + 2):
             j, i = divmod(s, TILES)
-            count = HALVES[s] if s < len(HALVES) else 0
-            previous = halves
-            halves = [divmod(h, 2 * PASSES) for h in range(done, done + count)]
+            count = UNITS[s] if s < len(UNITS) else 0
+            previous = units
+            units = [divmod(h, PASSES) for h in range(done, done + count)]
             done = done + count
-            share = SHARES[0 if s + 1 < TILES - 1 else 1 + j] if count else 0
+            share = SHARES[j] if count else 0
 
-            if s + 1 < TILES:
-                for c in range(CHUNKS):
-                    drain_activations(s + 1, c)
-            if s % 2 == 0 and 0 <= (s - 6) // 2 < STEPS // 2:
-                drain_y((s - 6) // 2)
+            if s + LEAD < TILES:
+                drain_history(s + LEAD, 0)
+                drain_history(s + LEAD, 1)
+            if 4 <= s + 3 < TILES:
+                drain_context(s + 3)
+            if s % 2 == 0 and s >= 6:
+                drain_y(s - 6, 2)
+            if i == TILES - 1 and plain(s + 1):
+                drain_bias(j + 1)
 
-            if s < STEPS:
-                multiply(s, "logits", 0, CTX_PASSES)
-                multiply(s, "implicit", CTX_PASSES, PASSES)
-            if s % 2 == 1 and 0 <= (s - 5) // 2 < STEPS // 2:
-                turn_y((s - 5) // 2)
-            if i == TILES - 2 and j + 1 < GROUPS:
-                spread_bias(j + 1)
-            if s + 2 < TILES:
-                for c in range(CHUNKS):
-                    turn_activations(s + 2, c)
-
-            if s + 4 < TILES:
-                load_context(s + 4)
-                load_history(s + 4)
-            if i in (1, 5) and s + 3 < STEPS:
-                load_user(*divmod((s + 3) // 4, 2))
-            while loaded < 2 * PASSES and loaded < done // 2 + W_LEAD:
-                load_weight(1 + loaded // PASSES, loaded % PASSES)
-                loaded = loaded + 1
-            if 0 <= s - STORE_LAG < STEPS:
-                store_y(s - STORE_LAG)
-            if s % 4 == 1 and 0 <= (s - 9) // 4 < 2 * GROUPS:
-                store_codes(*divmod((s - 9) // 4, 2))
-                if (s - 9) // 4 % 2 == 1:
-                    store_scales((s - 9) // 8)
-
-            if 0 <= s - 1 < STEPS:
-                add_bias(s - 1)
-            if 0 <= s - 3 < STEPS:
-                round_y(s - 3)
-            if 0 <= s - 2 < STEPS:
+            if 0 <= s - 2:
                 apply_gate(s - 2)
+                if s - 2 == last:
+                    break
+                if ROUND[(s - 2) // TILES] == "pool":
+                    round_y(s - 2, "pool")
             if 0 <= s - 1 < STEPS:
                 add_user(s - 1)
-                sigmoid(s - 1)
-            for jj, h in previous:
-                quantize_weight(jj + 1, h)
-            if s + 1 < TILES:
-                for c in range(CHUNKS):
-                    quantize_activations(s + 1, c)
-            if s % 2 == 0 and 0 <= (s - 6) // 2 < STEPS // 2:
-                quantize_y((s - 6) // 2)
-            for jj, h in halves:
-                interleave_vector(jj + 1, h, share)
-                interleave_scalar(jj + 1, h, share)
+            if plain(s):
+                add_bias(s)
+            if s >= 2 and ROUND[(s - 2) // TILES] == "scalar":
+                round_y(s - 2, "scalar")
+            if plain(s):
+                sigmoid(s)
+            if turned(s + 1):
+                sigmoid_turned(s + 1)
+
+            if s < STEPS:
+                multiply_implicit(s)
+            if plain(s + 1):
+                multiply_logits(s + 1)
+            if turned(s + 2):
+                multiply_logits_turned(s + 2)
+            if s % 2 == 1 and s >= 5:
+                turn_y(s - 5, 2)
+            if s == STEPS:
+                turn_y(s - 4, 2)
+            if s % 2 == 1 and turned(s):
+                turn_gate(s - 1)
+                turn_gate(s)
+            if i == TILES - 2 and plain(s + 2):
+                spread_bias(j + 1)
+            if s + LEAD + 1 < TILES:
+                turn_history(s + LEAD + 1, 0)
+                turn_history(s + LEAD + 1, 1)
+            if s + 4 < TILES:
+                turn_context(s + 4)
+
+            if s + 4 < TILES:
+                load_history(s + 4)
+            if s == C3:
+                load_context(3)
+            if s % 2 == 0 and s + 2 < STEPS:
+                load_user(s // 2 + 1)
+            while loaded < 2 * PASSES and loaded < done + W_LEAD:
+                load_weight(1 + loaded // PASSES, loaded % PASSES)
+                loaded = loaded + 1
+            if 0 <= s - STORE_LAG:
+                store_y(s - STORE_LAG)
+            if s % 4 == 1 and s >= 9:
+                jj, half = divmod((s - 9) // 4, 2)
+                store_codes(jj, 4 * half, 4 * half + 4)
+                if half == 1:
+                    store_scales(jj, [nc.sync])
+
+            if s + LEAD < TILES:
+                quantize_history(s + LEAD)
+            if 4 <= s + 3 < TILES:
+                quantize_context(s + 3)
+            if s % 2 == 0 and s >= 6:
+                quantize_y(s - 6, 2)
+            for jj, g in previous:
+                quantize_weight(jj + 1, g, 0, NG)
+            for jj, g in units:
+                interleave_vector(jj + 1, g, 0, share)
+                interleave_scalar(jj + 1, g, share, NG)
+
+        drain_y(last - 3, 2)
+        turn_y(last - 1, 1)
+        round_y(last, "vector")
+        for s in range(STEPS + 1 - STORE_LAG, STEPS):
+            store_y(s)
+        store_codes(GROUPS - 1, 0, 4)
+        drain_y(last - 1, 1)
+        turn_y(last, 1)
+        quantize_y(last - 3, 2)
+        quantize_y(last - 1, 1)
+        store_codes(GROUPS - 1, 4, 7)
+        drain_y(last, 1)
+        quantize_y(last, 1)
+        store_codes(GROUPS - 1, 7, 8)
+        store_scales(GROUPS - 1, [nc.sync, nc.scalar])

@@ -25,57 +25,61 @@ GROUPS = N // NG
 TILES = T // P
 STEPS = GROUPS * TILES
 CTX_PASSES = D // K_PASS
-PASSES = (D + I) // K_PASS
-CHUNKS = PASSES // 2
+ITEM_PASSES = I // K_PASS
+PASSES = CTX_PASSES + ITEM_PASSES
+BIAS_ROWS = N // P
+QUAD = 4
+
 HEAD_SHARE = 144
-SHARES = (288, 288)
-UNITS = (0, 1, 1, 1, 1, 1, 1, 0, 1, 1, 1, 1, 1, 0, 1, 0)
-TURNED = (1,)
-HEAD_LOADS = "w00 w01 c0 w02 h0 w03 c1 w04 h1 w05 h2 u c2 h3 w10"
-HEAD_JOBS = ("", "b", "c0", "h0 l", "c1", "")
-LEAD = 1
-C3 = 0
-ROUND = ("scalar", "scalar", "scalar")
+SHARES = (288, 192)
+
+TURN_BANKS = 4
+HISTORY_AHEAD = 4
+WEIGHTS_AHEAD = 2
 STORE_LAG = 4
-W_LEAD = 2
+
+
+def block(c):
+    return slice(c * P, (c + 1) * P)
 
 
 def tile_svdpp_context_gate_g1_kernel(
     tc, history, item_factors, context, w_context, b_context, user_factors, out_0, out_1, out_2
 ):
     nc = tc.nc
-    with ExitStack() as ctx:
-        keep = ctx.enter_context(tc.tile_pool(name="keep", bufs=1))
-        ring = ctx.enter_context(tc.tile_pool(name="ring", bufs=2))
-        psum = ctx.enter_context(tc.psum_pool(name="psum", bufs=2))
-        ctx.enter_context(tc.manual_schedule())
+    with ExitStack() as stack:
+        keep = stack.enter_context(tc.tile_pool(name="keep", bufs=1))
+        ring = stack.enter_context(tc.tile_pool(name="ring", bufs=2))
+        psum = stack.enter_context(tc.psum_pool(name="psum", bufs=2))
+        stack.enter_context(tc.manual_schedule())
 
         tiles = {}
 
         ident = keep.tile([P, P], F32, name="ident")
         make_identity(nc, ident[:])
 
+
         def load_bias():
-            b_rows = keep.tile([N // P, P], BF16, name="b_rows")
-            nc.scalar.dma_start(out=b_rows[:], in_=b_context.rearrange("(c p) -> c p", p=P))
+            b_rows = keep.tile([BIAS_ROWS, P], BF16, name="b_rows")
+            nc.sync.dma_start(out=b_rows[:], in_=b_context.rearrange("(c p) -> c p", p=P))
             tiles["b_rows"] = b_rows
 
         def turn_bias():
             b_wide = keep.tile([P, P], F32, name="b_wide")
             nc.gpsimd.memset(b_wide[:], 0.0)
-            nc.vector.tensor_copy(out=b_wide[0 : N // P, :], in_=tiles["b_rows"][:])
-            bank = psum.tile([P, P], F32, name="turn", bufs=4)
+            nc.vector.tensor_copy(out=b_wide[0:BIAS_ROWS, :], in_=tiles["b_rows"][:])
+            bank = psum.tile([P, P], F32, name="turn", bufs=TURN_BANKS)
             nc.tensor.transpose(bank[:], b_wide[:], ident[:])
-            b_cols = keep.tile([P, N // P], F32, name="b_cols")
-            nc.vector.tensor_copy(out=b_cols[:], in_=bank[:, 0 : N // P])
+            b_cols = keep.tile([P, BIAS_ROWS], F32, name="b_cols")
+            nc.vector.tensor_copy(out=b_cols[:], in_=bank[:, 0:BIAS_ROWS])
             tiles["b_cols"] = b_cols
 
         def spread_bias(j):
-            bank = psum.tile([P, NG], F32, name="turn", bufs=4)
-            for c in range(PACK):
-                col = PACK * j + c
+            bank = psum.tile([P, NG], F32, name="turn", bufs=TURN_BANKS)
+            for c in range(NG // P):
+                col = j * NG // P + c
                 nc.tensor.transpose(
-                    bank[:, c * P : (c + 1) * P], tiles["b_cols"][:, col : col + 1].to_broadcast([P, P]), ident[:]
+                    bank[:, block(c)], tiles["b_cols"][:, col : col + 1].to_broadcast([P, P]), ident[:]
                 )
             tiles["bias_bank", j] = bank
 
@@ -88,67 +92,60 @@ def tile_svdpp_context_gate_g1_kernel(
             warm = keep.tile([P, 1], F32, name="warm")
             nc.scalar.activation(out=warm[:], in_=ident[:, 0:1], func=SIGMOID)
 
+
         def load_context(q):
             raw = ring.tile([P, 2, D], BF16, name="ctx_raw", bufs=3)
             nc.sync.dma_start(out=raw[:], in_=context[q * 2 * P : (q + 1) * 2 * P, :].rearrange("(a p) k -> p a k", p=P))
             tiles["ctx_raw", q] = raw
 
         def load_history(i):
-            raw = ring.tile([P, I], BF16, name="hist_raw", bufs=4)
-            nc.sync.dma_start(out=raw[:], in_=history[i * P : (i + 1) * P, :])
+            raw = ring.tile([P, I], BF16, name="hist_raw", bufs=HISTORY_AHEAD)
+            nc.sync.dma_start(out=raw[:], in_=history[block(i), :])
             tiles["hist_raw", i] = raw
 
         def load_weight(j, g):
-            src = w_context if g < CTX_PASSES else item_factors
-            k0 = (g if g < CTX_PASSES else g - CTX_PASSES) * K_PASS
+            src, first = (w_context, g) if g < CTX_PASSES else (item_factors, g - CTX_PASSES)
             raw = ring.tile([P, PACK, NG], BF16, name="w_raw", bufs=8)
             nc.sync.dma_start(
                 out=raw[:],
-                in_=src[k0 : k0 + K_PASS, j * NG : (j + 1) * NG].rearrange("(p t) n -> p t n", t=PACK),
+                in_=src[first * K_PASS : (first + 1) * K_PASS, j * NG : (j + 1) * NG].rearrange(
+                    "(p t) n -> p t n", t=PACK
+                ),
             )
             tiles["w_raw", j, g] = raw
 
-        def load_user(q):
-            j, i = divmod(2 * q, TILES)
+        def load_user(pair):
+            j, i = divmod(2 * pair, TILES)
             raw = ring.tile([P, 2, NG], BF16, name="user", bufs=4)
             nc.sync.dma_start(
                 out=raw[:],
                 in_=user_factors[i * P : (i + 2) * P, j * NG : (j + 1) * NG].rearrange("(a p) n -> p a n", p=P),
             )
-            tiles["user", q] = raw
+            tiles["user", pair] = raw
 
-        def turn_words(key, sources):
-            bank = psum.tile([P, 2, 2, P], F32, name="turn", bufs=4)
+
+        def turn_pairs(key, sources):
+            bank = psum.tile([P, 2, 2, P], F32, name="turn", bufs=TURN_BANKS)
             for a in range(2):
                 for u in range(2):
-                    nc.tensor.transpose(bank[:, a, u, :], sources[a][:, u : 2 * P : 2], ident[:])
+                    nc.tensor.transpose(bank[:, a, u, :], sources[a].bitcast(F32)[:, u : 2 * P : 2], ident[:])
             tiles[key] = bank
+
+        def drain_pairs(bank, grouped, count):
+            nc.scalar.copy(
+                out=grouped.bitcast(F32).rearrange("p (a r u) -> p a r u", a=count, u=2),
+                in_=bank[:].rearrange("p a u r -> p a r u"),
+            )
 
         def turn_context(c):
             q, g = divmod(c, CTX_PASSES)
             raw = tiles["ctx_raw", q]
-            turn_words(("ctx_bank", c), [raw[:, a, g * K_PASS : (g + 1) * K_PASS].bitcast(F32) for a in range(2)])
-
-        def turn_history(i, c):
-            raw = tiles["hist_raw", i]
-            passes = (2 * c, 2 * c + 1)
-            turn_words(("hist_bank", i, c), [raw[:, g * K_PASS : (g + 1) * K_PASS].bitcast(F32) for g in passes])
-
-        def drain(bank, grouped):
-            nc.scalar.copy(
-                out=grouped.bitcast(F32).rearrange("p (a r u) -> p a r u", a=2, u=2),
-                in_=bank[:].rearrange("p a u r -> p a r u"),
-            )
+            turn_pairs(("ctx_bank", c), [raw[:, a, g * K_PASS : (g + 1) * K_PASS] for a in range(2)])
 
         def drain_context(c):
             grouped = ring.tile([P, 2 * K_PASS], BF16, name="ctx_grouped", bufs=3, align_bytes=64)
-            drain(tiles["ctx_bank", c], grouped[:])
+            drain_pairs(tiles["ctx_bank", c], grouped[:], 2)
             tiles["ctx_grouped", c] = grouped
-
-        def drain_history(i, c):
-            if c == 0:
-                tiles["hist_grouped", i] = ring.tile([P, I], BF16, name="hist_grouped", bufs=2, align_bytes=64)
-            drain(tiles["hist_bank", i, c], tiles["hist_grouped", i][:, c * 2 * K_PASS : (c + 1) * 2 * K_PASS])
 
         def quantize_context(c):
             codes = keep.tile([P, 2 * P], U32, name="ctx_codes%d" % c, align_bytes=64)
@@ -156,25 +153,30 @@ def tile_svdpp_context_gate_g1_kernel(
             nc.vector.quantize_mx(out=codes[:].bitcast(FP8X4), scales=scales[:], in_=tiles["ctx_grouped", c][:])
             tiles["ctx_mx", c] = (codes, scales)
 
+        def turn_history(i, h):
+            raw = tiles["hist_raw", i]
+            turn_pairs(("hist_bank", i, h), [raw[:, g * K_PASS : (g + 1) * K_PASS] for g in (2 * h, 2 * h + 1)])
+
+        def drain_history(i, h):
+            if h == 0:
+                tiles["hist_grouped", i] = ring.tile([P, I], BF16, name="hist_grouped", align_bytes=64)
+            drain_pairs(tiles["hist_bank", i, h], tiles["hist_grouped", i][:, h * 2 * K_PASS : (h + 1) * 2 * K_PASS], 2)
+
         def quantize_history(i):
-            codes = keep.tile([P, 4 * P], U32, name="hist_codes%d" % i, align_bytes=64)
-            scales = keep.tile([P, 4 * P], U8, name="hist_scales%d" % i, align_bytes=64)
+            codes = keep.tile([P, ITEM_PASSES * P], U32, name="hist_codes%d" % i, align_bytes=64)
+            scales = keep.tile([P, ITEM_PASSES * P], U8, name="hist_scales%d" % i, align_bytes=64)
             nc.vector.quantize_mx(out=codes[:].bitcast(FP8X4), scales=scales[:], in_=tiles["hist_grouped", i][:])
             tiles["hist_mx", i] = (codes, scales)
 
-        def interleave(copy, j, g, c0, c1):
-            if ("w_grouped", j, g) not in tiles:
+
+        def interleave_weight(j, g, c0, split, c1):
+            if c0 == 0:
                 tiles["w_grouped", j, g] = ring.tile([P, NG, PACK], BF16, name="w_grouped", bufs=3, align_bytes=64)
-            copy(
-                out=tiles["w_grouped", j, g][:, c0:c1, :].rearrange("p (c i) t -> p c t i", i=4),
-                in_=tiles["w_raw", j, g][:, :, c0:c1].rearrange("p t (c i) -> p c t i", i=4),
-            )
-
-        def interleave_vector(j, g, c0, c1):
-            interleave(nc.vector.tensor_copy, j, g, c0, c1)
-
-        def interleave_scalar(j, g, c0, c1):
-            interleave(nc.scalar.copy, j, g, c0, c1)
+            for copy, cols in ((nc.vector.tensor_copy, slice(c0, split)), (nc.scalar.copy, slice(split, c1))):
+                copy(
+                    out=tiles["w_grouped", j, g][:, cols, :].rearrange("p (c i) t -> p c t i", i=4),
+                    in_=tiles["w_raw", j, g][:, :, cols].rearrange("p t (c i) -> p c t i", i=4),
+                )
 
         def quantize_weight(j, g, c0, c1):
             if c0 == 0:
@@ -188,72 +190,32 @@ def tile_svdpp_context_gate_g1_kernel(
                 in_=tiles["w_grouped", j, g][:, c0:c1, :].rearrange("p n t -> p (n t)"),
             )
 
-        def mx_group(out, passes):
-            for g, (stationary, s_cols, moving) in enumerate(passes):
+
+        def mx_product(name, s, passes):
+            bank = psum.tile([P, NG], F32, name=name)
+            for g, (activations, users, weights) in enumerate(passes):
                 nc.tensor.matmul_mx(
-                    out=out,
-                    lhsT=stationary[0][:, s_cols].bitcast(FP8X4),
-                    lhsT_scale=stationary[1][:, s_cols],
-                    rhs=moving[0][:].bitcast(FP8X4),
-                    rhs_scale=moving[1][:],
+                    out=bank[:],
+                    lhsT=activations[0][:, users].bitcast(FP8X4),
+                    lhsT_scale=activations[1][:, users],
+                    rhs=weights[0][:].bitcast(FP8X4),
+                    rhs_scale=weights[1][:],
                     start=(g == 0),
                     stop=(g == len(passes) - 1),
                 )
-
-        def block(c):
-            return slice(c * P, (c + 1) * P)
+            tiles[name, s] = bank
 
         def multiply_logits(s):
             j, i = divmod(s, TILES)
-            bank = psum.tile([P, NG], F32, name="logits")
             q, a = divmod(i, 2)
-            mx_group(
-                bank[:],
-                [(tiles["ctx_mx", CTX_PASSES * q + g], block(a), tiles["w_mx", j, g]) for g in range(CTX_PASSES)],
-            )
-            tiles["logits", s] = bank
+            passes = [(tiles["ctx_mx", CTX_PASSES * q + g], block(a), tiles["w_mx", j, g]) for g in range(CTX_PASSES)]
+            mx_product("logits", s, passes)
 
         def multiply_implicit(s):
             j, i = divmod(s, TILES)
-            bank = psum.tile([P, NG], F32, name="implicit")
-            mx_group(
-                bank[:],
-                [(tiles["hist_mx", i], block(g), tiles["w_mx", j, CTX_PASSES + g]) for g in range(PASSES - CTX_PASSES)],
-            )
-            tiles["implicit", s] = bank
+            passes = [(tiles["hist_mx", i], block(g), tiles["w_mx", j, CTX_PASSES + g]) for g in range(ITEM_PASSES)]
+            mx_product("implicit", s, passes)
 
-        def multiply_logits_turned(s):
-            j, i = divmod(s, TILES)
-            q, b = divmod(i, 2)
-            bank = psum.tile([P, 2, 2 * P], F32, name="logits")
-            for c in range(2):
-                mx_group(
-                    bank[:, c, :],
-                    [
-                        (tiles["w_mx", j, g], block(2 * b + c), tiles["ctx_mx", CTX_PASSES * q + g])
-                        for g in range(CTX_PASSES)
-                    ],
-                )
-            tiles["logits_t", s] = bank
-
-        def sigmoid_turned(s):
-            j, b = s // TILES, s % 2
-            if b == 0:
-                tiles["gate_t", s // 2] = ring.tile([P, PACK, 2 * P], F32, name="gate_t")
-            for c in range(2):
-                col = PACK * j + 2 * b + c
-                nc.scalar.activation(
-                    out=tiles["gate_t", s // 2][:, 2 * b + c, :],
-                    in_=tiles["logits_t", s][:, c, :],
-                    func=SIGMOID,
-                    bias=tiles["b_cols"][:, col : col + 1],
-                )
-
-        def turn_gate(s):
-            bank = psum.tile([P, NG], F32, name="turn", bufs=4)
-            for c in range(PACK):
-                nc.tensor.transpose(bank[:, block(c)], tiles["gate_t", s // 2][:, c, block(s % 2)], ident[:])
-            tiles["gate", s] = bank
 
         def add_bias(s):
             z = ring.tile([P, NG], F32, name="z")
@@ -277,32 +239,26 @@ def tile_svdpp_context_gate_g1_kernel(
             nc.vector.tensor_tensor(out=y[:], in0=tiles["total", s][:], in1=tiles["gate", s][:], op=MULT)
             tiles["y", s] = y
 
-        def round_y(s, engine):
-            y_bf = ring.tile([P, NG], BF16, name="y_bf", bufs=4)
-            dst = y_bf[:].rearrange("m (u p e) -> m u p e", u=2, e=2)
-            src = tiles["y", s][:].rearrange("m (p u e) -> m u p e", u=2, e=2)
-            if engine == "pool":
-                nc.gpsimd.tensor_scalar(out=dst, in0=src, scalar1=1.0, scalar2=0.0, op0=MULT, op1=ADD)
-            elif engine == "vector":
-                nc.vector.tensor_copy(out=dst, in_=src)
-            else:
-                nc.scalar.copy(out=dst, in_=src)
+
+        def round_y(s, copy):
+            y_bf = ring.tile([P, NG], BF16, name="y_bf", bufs=QUAD + 2)
+            copy(
+                out=y_bf[:].rearrange("m (u p e) -> m u p e", u=2, e=2),
+                in_=tiles["y", s][:].rearrange("m (p u e) -> m u p e", u=2, e=2),
+            )
             tiles["y_bf", s] = y_bf
 
         def turn_y(s, count):
-            bank = psum.tile([P, count, 2, P], F32, name="turn", bufs=4)
+            bank = psum.tile([P, count, 2, P], F32, name="turn", bufs=TURN_BANKS)
             for a in range(count):
-                words = tiles["y_bf", s + a][:].bitcast(F32)
+                pairs = tiles["y_bf", s + a][:].bitcast(F32)
                 for u in range(2):
-                    nc.tensor.transpose(bank[:, a, u, :], words[:, block(u)], ident[:])
+                    nc.tensor.transpose(bank[:, a, u, :], pairs[:, block(u)], ident[:])
             tiles["y_bank", s] = bank
 
         def drain_y(s, count):
             grouped = ring.tile([P, count * K_PASS], BF16, name="y_grouped", align_bytes=64)
-            nc.scalar.copy(
-                out=grouped[:].bitcast(F32).rearrange("p (a r u) -> p a r u", a=count, u=2),
-                in_=tiles["y_bank", s][:].rearrange("p a u r -> p a r u"),
-            )
+            drain_pairs(tiles["y_bank", s], grouped[:], count)
             tiles["y_grouped", s] = grouped
 
         def quantize_y(s, count):
@@ -312,19 +268,20 @@ def tile_svdpp_context_gate_g1_kernel(
                 scales = ring.tile([P, T], U8, name="y_scales", align_bytes=64)
                 tiles["y_mx", j] = (codes, scales)
             codes, scales = tiles["y_mx", j]
-            cols = slice(i * P, (i + count) * P)
+            users = slice(i * P, (i + count) * P)
             nc.vector.quantize_mx(
-                out=codes[:, cols].bitcast(FP8X4), scales=scales[:, cols], in_=tiles["y_grouped", s][:]
+                out=codes[:, users].bitcast(FP8X4), scales=scales[:, users], in_=tiles["y_grouped", s][:]
             )
+
 
         def store_y(s):
             j, i = divmod(s, TILES)
-            nc.sync.dma_start(out=out_0[i * P : (i + 1) * P, j * NG : (j + 1) * NG], in_=tiles["y", s][:])
+            nc.sync.dma_start(out=out_0[block(i), j * NG : (j + 1) * NG], in_=tiles["y", s][:])
 
         def store_codes(j, i0, i1):
-            cols = slice(i0 * P, i1 * P)
+            users = slice(i0 * P, i1 * P)
             words = out_1[j].rearrange("p m t -> p (m t)").bitcast(I32)
-            nc.sync.dma_start(out=words[:, cols], in_=tiles["y_mx", j][0][:, cols].bitcast(I32))
+            nc.sync.dma_start(out=words[:, users], in_=tiles["y_mx", j][0][:, users].bitcast(I32))
 
         def store_scales(j, queues):
             scales = tiles["y_mx", j][1]
@@ -333,159 +290,153 @@ def tile_svdpp_context_gate_g1_kernel(
                     out=out_2[j, 4 * q : 4 * q + 4, :].bitcast(I32), in_=scales[32 * q : 32 * q + 4, :].bitcast(I32)
                 )
 
-        def turned(s):
-            return 0 <= s < STEPS and s // TILES in TURNED
-
-        def plain(s):
-            return 0 <= s < STEPS and s // TILES not in TURNED
-
+        load_weight(0, 0)
+        load_weight(0, 1)
         load_bias()
-        for name in HEAD_LOADS.split():
-            if name[0] == "w":
-                load_weight(int(name[1]), int(name[2]))
-            elif name[0] == "c":
-                load_context(int(name[1]))
-            elif name[0] == "h":
-                load_history(int(name[1]))
+        for g in range(2, PASSES):
+            q, is_history = divmod(g - 2, 2)
+            if is_history:
+                load_history(q)
             else:
-                load_user(0)
+                load_context(q)
+            load_weight(0, g)
+        load_history(2)
+        load_user(0)
+        load_context(2)
+        load_history(3)
+        load_weight(1, 0)
         warm_sigmoid()
+
+        def prepare_head_weight(g):
+            interleave_weight(0, g, 0, HEAD_SHARE, HALF)
+            if g >= 1:
+                quantize_weight(0, g - 1, HALF, NG)
+            interleave_weight(0, g, HALF, HALF + HEAD_SHARE, NG)
+            quantize_weight(0, g, 0, HALF)
+
+        def turn_and_drain_context(q):
+            for c in (2 * q, 2 * q + 1):
+                turn_context(c)
+                drain_context(c)
+
+        prepare_head_weight(0)
         turn_bias()
-        for g in range(PASSES):
-            jobs = HEAD_JOBS[g].split()
-            for name in jobs:
-                if name[0] == "c":
-                    for c in (2 * int(name[1]), 2 * int(name[1]) + 1):
-                        turn_context(c)
-                        drain_context(c)
-                elif name[0] == "h":
-                    for c in range(2):
-                        turn_history(int(name[1]), c)
-                        drain_history(int(name[1]), c)
-                elif name[0] == "l":
-                    multiply_logits(0)
-                else:
-                    spread_bias(0)
-                    drain_bias(0)
-            for half in range(2):
-                c0 = half * HALF
-                interleave_vector(0, g, c0, c0 + HEAD_SHARE)
-                interleave_scalar(0, g, c0 + HEAD_SHARE, c0 + HALF)
-                if half == 1:
-                    quantize_weight(0, g, 0, HALF)
-                elif g >= 1:
-                    quantize_weight(0, g - 1, HALF, NG)
-            for name in jobs:
-                if name[0] == "c":
-                    quantize_context(2 * int(name[1]))
-                    quantize_context(2 * int(name[1]) + 1)
-                elif name[0] == "h":
-                    quantize_history(int(name[1]))
+        prepare_head_weight(1)
+        spread_bias(0)
+        drain_bias(0)
+        turn_and_drain_context(0)
+        prepare_head_weight(2)
+        quantize_context(0)
+        quantize_context(1)
+        for h in range(2):
+            turn_history(0, h)
+            drain_history(0, h)
+        multiply_logits(0)
+        prepare_head_weight(3)
+        quantize_history(0)
+        turn_and_drain_context(1)
+        prepare_head_weight(4)
+        quantize_context(2)
+        quantize_context(3)
+        prepare_head_weight(5)
         quantize_weight(0, PASSES - 1, HALF, NG)
-        turn_history(LEAD, 0)
-        turn_history(LEAD, 1)
+        for h in range(2):
+            turn_history(1, h)
 
-        done = 0
-        loaded = 1
-        units = []
-        last = STEPS - 1
-        for s in range(STEPS + 2):
+        def weight_pass(s):
             j, i = divmod(s, TILES)
-            count = UNITS[s] if s < len(UNITS) else 0
-            previous = units
-            units = [divmod(h, PASSES) for h in range(done, done + count)]
-            done = done + count
-            share = SHARES[j] if count else 0
+            return (j + 1, i - 1) if j + 1 < GROUPS and 1 <= i <= PASSES else None
 
-            if s + LEAD < TILES:
-                drain_history(s + LEAD, 0)
-                drain_history(s + LEAD, 1)
+        last = STEPS - 1
+        loaded = 1
+        interleaved = 0
+        for s in range(STEPS + 1):
+            j, i = divmod(s, TILES)
+            y_pair = s - 2 * QUAD + s % QUAD if s >= 2 * QUAD and s % QUAD < 2 else None
+
+            if s + 1 < TILES:
+                for h in range(2):
+                    drain_history(s + 1, h)
             if 4 <= s + 3 < TILES:
                 drain_context(s + 3)
-            if s % 2 == 0 and s >= 6:
-                drain_y(s - 6, 2)
-            if i == TILES - 1 and plain(s + 1):
+            if y_pair is not None:
+                drain_y(y_pair, 2)
+            if i == TILES - 1 and j + 1 < GROUPS:
                 drain_bias(j + 1)
 
-            if 0 <= s - 2:
+            if s >= 2:
                 apply_gate(s - 2)
-                if s - 2 == last:
-                    break
-                if ROUND[(s - 2) // TILES] == "pool":
-                    round_y(s - 2, "pool")
-            if 0 <= s - 1 < STEPS:
+            if s >= 1:
                 add_user(s - 1)
-            if plain(s):
+            if s < STEPS:
                 add_bias(s)
-            if s >= 2 and ROUND[(s - 2) // TILES] == "scalar":
-                round_y(s - 2, "scalar")
-            if plain(s):
+            if s >= 2:
+                round_y(s - 2, nc.scalar.copy)
+            if s < STEPS:
                 sigmoid(s)
-            if turned(s + 1):
-                sigmoid_turned(s + 1)
 
             if s < STEPS:
                 multiply_implicit(s)
-            if plain(s + 1):
+            if s + 1 < STEPS:
                 multiply_logits(s + 1)
-            if turned(s + 2):
-                multiply_logits_turned(s + 2)
-            if s % 2 == 1 and s >= 5:
-                turn_y(s - 5, 2)
+            if s >= 2 * QUAD - 1 and s % QUAD == QUAD - 1:
+                turn_y(s - 2 * QUAD + 1, 2)
+                turn_y(s - 2 * QUAD + 3, 2)
             if s == STEPS:
-                turn_y(s - 4, 2)
-            if s % 2 == 1 and turned(s):
-                turn_gate(s - 1)
-                turn_gate(s)
-            if i == TILES - 2 and plain(s + 2):
+                turn_y(last - 3, 2)
+            if i == TILES - 2 and j + 1 < GROUPS:
                 spread_bias(j + 1)
-            if s + LEAD + 1 < TILES:
-                turn_history(s + LEAD + 1, 0)
-                turn_history(s + LEAD + 1, 1)
+            if s + 2 < TILES:
+                for h in range(2):
+                    turn_history(s + 2, h)
             if s + 4 < TILES:
                 turn_context(s + 4)
 
-            if s + 4 < TILES:
-                load_history(s + 4)
-            if s == C3:
+            if s + HISTORY_AHEAD < TILES:
+                load_history(s + HISTORY_AHEAD)
+            if s == 0:
                 load_context(3)
             if s % 2 == 0 and s + 2 < STEPS:
                 load_user(s // 2 + 1)
-            while loaded < 2 * PASSES and loaded < done + W_LEAD:
+            if weight_pass(s):
+                interleaved = interleaved + 1
+            while loaded < min(interleaved + WEIGHTS_AHEAD, (GROUPS - 1) * PASSES):
                 load_weight(1 + loaded // PASSES, loaded % PASSES)
                 loaded = loaded + 1
-            if 0 <= s - STORE_LAG:
+            if s >= STORE_LAG:
                 store_y(s - STORE_LAG)
-            if s % 4 == 1 and s >= 9:
-                jj, half = divmod((s - 9) // 4, 2)
-                store_codes(jj, 4 * half, 4 * half + 4)
-                if half == 1:
-                    store_scales(jj, [nc.sync])
+            if s >= 3 * QUAD - 1 and s % QUAD == QUAD - 1:
+                done_j, done_i = divmod(s - 3 * QUAD + 1, TILES)
+                store_codes(done_j, done_i, done_i + QUAD)
+                if done_i + QUAD == TILES:
+                    store_scales(done_j, [nc.sync])
 
-            if s + LEAD < TILES:
-                quantize_history(s + LEAD)
+            if s + 1 < TILES:
+                quantize_history(s + 1)
             if 4 <= s + 3 < TILES:
                 quantize_context(s + 3)
-            if s % 2 == 0 and s >= 6:
-                quantize_y(s - 6, 2)
-            for jj, g in previous:
-                quantize_weight(jj + 1, g, 0, NG)
-            for jj, g in units:
-                interleave_vector(jj + 1, g, 0, share)
-                interleave_scalar(jj + 1, g, share, NG)
+            if s >= 1 and weight_pass(s - 1):
+                quantize_weight(*weight_pass(s - 1), 0, NG)
+            if weight_pass(s):
+                interleave_weight(*weight_pass(s), 0, SHARES[j], NG)
+            if y_pair is not None:
+                quantize_y(y_pair, 2)
 
+        drain_y(last - 5, 2)
+        apply_gate(last)
+        quantize_y(last - 5, 2)
         drain_y(last - 3, 2)
         turn_y(last - 1, 1)
-        round_y(last, "vector")
+        round_y(last, nc.vector.tensor_copy)
         for s in range(STEPS + 1 - STORE_LAG, STEPS):
             store_y(s)
-        store_codes(GROUPS - 1, 0, 4)
+        store_codes(GROUPS - 1, 0, QUAD)
         drain_y(last - 1, 1)
         turn_y(last, 1)
         quantize_y(last - 3, 2)
         quantize_y(last - 1, 1)
-        store_codes(GROUPS - 1, 4, 7)
+        store_codes(GROUPS - 1, QUAD, TILES - 1)
         drain_y(last, 1)
         quantize_y(last, 1)
-        store_codes(GROUPS - 1, 7, 8)
+        store_codes(GROUPS - 1, TILES - 1, TILES)
         store_scales(GROUPS - 1, [nc.sync, nc.scalar])

@@ -28,6 +28,8 @@ CTX_PASSES = D // K_PASS
 ITEM_PASSES = I // K_PASS
 PASSES = CTX_PASSES + ITEM_PASSES
 BIAS_ROWS = N // P
+CTX_CHUNKS = TILES // 2 * CTX_PASSES
+HEAD_CHUNKS = 2 * CTX_PASSES
 QUAD = 4
 
 HEAD_SHARE = 144
@@ -37,9 +39,10 @@ TURN_BANKS = 4
 HISTORY_AHEAD = 4
 WEIGHTS_AHEAD = 2
 STORE_LAG = 4
+W_RAW_BUFS = 8
 
 
-def block(c):
+def cols128(c):
     return slice(c * P, (c + 1) * P)
 
 
@@ -79,7 +82,7 @@ def tile_svdpp_context_gate_g1_kernel(
             for c in range(NG // P):
                 col = j * NG // P + c
                 nc.tensor.transpose(
-                    bank[:, block(c)], tiles["b_cols"][:, col : col + 1].to_broadcast([P, P]), ident[:]
+                    bank[:, cols128(c)], tiles["b_cols"][:, col : col + 1].to_broadcast([P, P]), ident[:]
                 )
             tiles["bias_bank", j] = bank
 
@@ -88,24 +91,21 @@ def tile_svdpp_context_gate_g1_kernel(
             nc.scalar.copy(out=bias[:], in_=tiles["bias_bank", j][:])
             tiles["bias", j] = bias
 
-        def warm_sigmoid():
-            warm = keep.tile([P, 1], F32, name="warm")
-            nc.scalar.activation(out=warm[:], in_=ident[:, 0:1], func=SIGMOID)
-
 
         def load_context(q):
             raw = ring.tile([P, 2, D], BF16, name="ctx_raw", bufs=3)
-            nc.sync.dma_start(out=raw[:], in_=context[q * 2 * P : (q + 1) * 2 * P, :].rearrange("(a p) k -> p a k", p=P))
+            rows = context[q * 2 * P : (q + 1) * 2 * P, :]
+            nc.sync.dma_start(out=raw[:], in_=rows.rearrange("(a p) k -> p a k", p=P))
             tiles["ctx_raw", q] = raw
 
         def load_history(i):
             raw = ring.tile([P, I], BF16, name="hist_raw", bufs=HISTORY_AHEAD)
-            nc.sync.dma_start(out=raw[:], in_=history[block(i), :])
+            nc.sync.dma_start(out=raw[:], in_=history[cols128(i), :])
             tiles["hist_raw", i] = raw
 
         def load_weight(j, g):
             src, first = (w_context, g) if g < CTX_PASSES else (item_factors, g - CTX_PASSES)
-            raw = ring.tile([P, PACK, NG], BF16, name="w_raw", bufs=8)
+            raw = ring.tile([P, PACK, NG], BF16, name="w_raw", bufs=W_RAW_BUFS)
             nc.sync.dma_start(
                 out=raw[:],
                 in_=src[first * K_PASS : (first + 1) * K_PASS, j * NG : (j + 1) * NG].rearrange(
@@ -114,14 +114,14 @@ def tile_svdpp_context_gate_g1_kernel(
             )
             tiles["w_raw", j, g] = raw
 
-        def load_user(pair):
-            j, i = divmod(2 * pair, TILES)
+        def load_user(s):
+            j, i = divmod(s, TILES)
             raw = ring.tile([P, 2, NG], BF16, name="user", bufs=4)
             nc.sync.dma_start(
                 out=raw[:],
                 in_=user_factors[i * P : (i + 2) * P, j * NG : (j + 1) * NG].rearrange("(a p) n -> p a n", p=P),
             )
-            tiles["user", pair] = raw
+            tiles["user", s // 2] = raw
 
 
         def turn_pairs(key, sources):
@@ -137,21 +137,21 @@ def tile_svdpp_context_gate_g1_kernel(
                 in_=bank[:].rearrange("p a u r -> p a r u"),
             )
 
-        def turn_context(c):
-            q, g = divmod(c, CTX_PASSES)
+        def turn_context(chunk):
+            q, g = divmod(chunk, CTX_PASSES)
             raw = tiles["ctx_raw", q]
-            turn_pairs(("ctx_bank", c), [raw[:, a, g * K_PASS : (g + 1) * K_PASS] for a in range(2)])
+            turn_pairs(("ctx_bank", chunk), [raw[:, a, g * K_PASS : (g + 1) * K_PASS] for a in range(2)])
 
-        def drain_context(c):
+        def drain_context(chunk):
             grouped = ring.tile([P, 2 * K_PASS], BF16, name="ctx_grouped", bufs=3, align_bytes=64)
-            drain_pairs(tiles["ctx_bank", c], grouped[:], 2)
-            tiles["ctx_grouped", c] = grouped
+            drain_pairs(tiles["ctx_bank", chunk], grouped[:], 2)
+            tiles["ctx_grouped", chunk] = grouped
 
-        def quantize_context(c):
-            codes = keep.tile([P, 2 * P], U32, name="ctx_codes%d" % c, align_bytes=64)
-            scales = keep.tile([P, 2 * P], U8, name="ctx_scales%d" % c, align_bytes=64)
-            nc.vector.quantize_mx(out=codes[:].bitcast(FP8X4), scales=scales[:], in_=tiles["ctx_grouped", c][:])
-            tiles["ctx_mx", c] = (codes, scales)
+        def quantize_context(chunk):
+            codes = keep.tile([P, 2 * P], U32, name="ctx_codes%d" % chunk, align_bytes=64)
+            scales = keep.tile([P, 2 * P], U8, name="ctx_scales%d" % chunk, align_bytes=64)
+            nc.vector.quantize_mx(out=codes[:].bitcast(FP8X4), scales=scales[:], in_=tiles["ctx_grouped", chunk][:])
+            tiles["ctx_mx", chunk] = (codes, scales)
 
         def turn_history(i, h):
             raw = tiles["hist_raw", i]
@@ -174,8 +174,8 @@ def tile_svdpp_context_gate_g1_kernel(
                 tiles["w_grouped", j, g] = ring.tile([P, NG, PACK], BF16, name="w_grouped", bufs=3, align_bytes=64)
             for copy, cols in ((nc.vector.tensor_copy, slice(c0, split)), (nc.scalar.copy, slice(split, c1))):
                 copy(
-                    out=tiles["w_grouped", j, g][:, cols, :].rearrange("p (c i) t -> p c t i", i=4),
-                    in_=tiles["w_raw", j, g][:, :, cols].rearrange("p t (c i) -> p c t i", i=4),
+                    out=tiles["w_grouped", j, g][:, cols, :].rearrange("p (run col) t -> p run t col", col=4),
+                    in_=tiles["w_raw", j, g][:, :, cols].rearrange("p t (run col) -> p run t col", col=4),
                 )
 
         def quantize_weight(j, g, c0, c1):
@@ -208,12 +208,12 @@ def tile_svdpp_context_gate_g1_kernel(
         def multiply_logits(s):
             j, i = divmod(s, TILES)
             q, a = divmod(i, 2)
-            passes = [(tiles["ctx_mx", CTX_PASSES * q + g], block(a), tiles["w_mx", j, g]) for g in range(CTX_PASSES)]
+            passes = [(tiles["ctx_mx", CTX_PASSES * q + g], cols128(a), tiles["w_mx", j, g]) for g in range(CTX_PASSES)]
             mx_product("logits", s, passes)
 
         def multiply_implicit(s):
             j, i = divmod(s, TILES)
-            passes = [(tiles["hist_mx", i], block(g), tiles["w_mx", j, CTX_PASSES + g]) for g in range(ITEM_PASSES)]
+            passes = [(tiles["hist_mx", i], cols128(g), tiles["w_mx", j, CTX_PASSES + g]) for g in range(ITEM_PASSES)]
             mx_product("implicit", s, passes)
 
 
@@ -253,7 +253,7 @@ def tile_svdpp_context_gate_g1_kernel(
             for a in range(count):
                 pairs = tiles["y_bf", s + a][:].bitcast(F32)
                 for u in range(2):
-                    nc.tensor.transpose(bank[:, a, u, :], pairs[:, block(u)], ident[:])
+                    nc.tensor.transpose(bank[:, a, u, :], pairs[:, cols128(u)], ident[:])
             tiles["y_bank", s] = bank
 
         def drain_y(s, count):
@@ -276,7 +276,7 @@ def tile_svdpp_context_gate_g1_kernel(
 
         def store_y(s):
             j, i = divmod(s, TILES)
-            nc.sync.dma_start(out=out_0[block(i), j * NG : (j + 1) * NG], in_=tiles["y", s][:])
+            nc.sync.dma_start(out=out_0[cols128(i), j * NG : (j + 1) * NG], in_=tiles["y", s][:])
 
         def store_codes(j, i0, i1):
             users = slice(i0 * P, i1 * P)
@@ -285,27 +285,27 @@ def tile_svdpp_context_gate_g1_kernel(
 
         def store_scales(j, queues):
             scales = tiles["y_mx", j][1]
-            for q in range(4):
-                queues[q % len(queues)].dma_start(
-                    out=out_2[j, 4 * q : 4 * q + 4, :].bitcast(I32), in_=scales[32 * q : 32 * q + 4, :].bitcast(I32)
+            for quadrant in range(4):
+                queues[quadrant % len(queues)].dma_start(
+                    out=out_2[j, 4 * quadrant : 4 * quadrant + 4, :].bitcast(I32),
+                    in_=scales[32 * quadrant : 32 * quadrant + 4, :].bitcast(I32),
                 )
 
         load_weight(0, 0)
         load_weight(0, 1)
         load_bias()
         for g in range(2, PASSES):
-            q, is_history = divmod(g - 2, 2)
+            index, is_history = divmod(g - 2, 2)
             if is_history:
-                load_history(q)
+                load_history(index)
             else:
-                load_context(q)
+                load_context(index)
             load_weight(0, g)
         load_history(2)
         load_user(0)
         load_context(2)
         load_history(3)
         load_weight(1, 0)
-        warm_sigmoid()
 
         def prepare_head_weight(g):
             interleave_weight(0, g, 0, HEAD_SHARE, HALF)
@@ -315,9 +315,9 @@ def tile_svdpp_context_gate_g1_kernel(
             quantize_weight(0, g, 0, HALF)
 
         def turn_and_drain_context(q):
-            for c in (2 * q, 2 * q + 1):
-                turn_context(c)
-                drain_context(c)
+            for chunk in (2 * q, 2 * q + 1):
+                turn_context(chunk)
+                drain_context(chunk)
 
         prepare_head_weight(0)
         turn_bias()
@@ -352,15 +352,15 @@ def tile_svdpp_context_gate_g1_kernel(
         interleaved = 0
         for s in range(STEPS + 1):
             j, i = divmod(s, TILES)
-            y_pair = s - 2 * QUAD + s % QUAD if s >= 2 * QUAD and s % QUAD < 2 else None
+            y_first = s - 2 * QUAD + s % QUAD if s >= 2 * QUAD and s % QUAD < 2 else None
 
             if s + 1 < TILES:
                 for h in range(2):
                     drain_history(s + 1, h)
-            if 4 <= s + 3 < TILES:
-                drain_context(s + 3)
-            if y_pair is not None:
-                drain_y(y_pair, 2)
+            if HEAD_CHUNKS <= s + HEAD_CHUNKS - 1 < CTX_CHUNKS:
+                drain_context(s + HEAD_CHUNKS - 1)
+            if y_first is not None:
+                drain_y(y_first, 2)
             if i == TILES - 1 and j + 1 < GROUPS:
                 drain_bias(j + 1)
 
@@ -389,15 +389,15 @@ def tile_svdpp_context_gate_g1_kernel(
             if s + 2 < TILES:
                 for h in range(2):
                     turn_history(s + 2, h)
-            if s + 4 < TILES:
-                turn_context(s + 4)
+            if s + HEAD_CHUNKS < CTX_CHUNKS:
+                turn_context(s + HEAD_CHUNKS)
 
             if s + HISTORY_AHEAD < TILES:
                 load_history(s + HISTORY_AHEAD)
             if s == 0:
-                load_context(3)
+                load_context(TILES // 2 - 1)
             if s % 2 == 0 and s + 2 < STEPS:
-                load_user(s // 2 + 1)
+                load_user(s + 2)
             if weight_pass(s):
                 interleaved = interleaved + 1
             while loaded < min(interleaved + WEIGHTS_AHEAD, (GROUPS - 1) * PASSES):
@@ -413,14 +413,14 @@ def tile_svdpp_context_gate_g1_kernel(
 
             if s + 1 < TILES:
                 quantize_history(s + 1)
-            if 4 <= s + 3 < TILES:
-                quantize_context(s + 3)
+            if HEAD_CHUNKS <= s + HEAD_CHUNKS - 1 < CTX_CHUNKS:
+                quantize_context(s + HEAD_CHUNKS - 1)
             if s >= 1 and weight_pass(s - 1):
                 quantize_weight(*weight_pass(s - 1), 0, NG)
             if weight_pass(s):
                 interleave_weight(*weight_pass(s), 0, SHARES[j], NG)
-            if y_pair is not None:
-                quantize_y(y_pair, 2)
+            if y_first is not None:
+                quantize_y(y_first, 2)
 
         drain_y(last - 5, 2)
         apply_gate(last)

from contextlib import ExitStack

import concourse.mybir as mybir
from concourse.masks import make_identity

T, I, D, N = 1024, 2048, 1024, 1536
FLOPS = 2 * T * (I + D) * N

F32 = mybir.dt.float32
BF16 = mybir.dt.bfloat16
U32 = mybir.dt.uint32
I32 = mybir.dt.int32
U8 = mybir.dt.uint8
FP8X4 = mybir.dt.float8_e4m3fn_x4
ADD = mybir.AluOpType.add
MULT = mybir.AluOpType.mult
SIGMOID = mybir.ActivationFunctionType.Sigmoid

P = 128
PACK = 4
K_PASS = P * PACK
NG = 512
HALF = NG // 2
GROUPS = N // NG
TILES = T // P
STEPS = GROUPS * TILES
CTX_PASSES = D // K_PASS
ITEM_PASSES = I // K_PASS
PASSES = CTX_PASSES + ITEM_PASSES
BIAS_ROWS = N // P
CTX_CHUNKS = TILES // 2 * CTX_PASSES
HEAD_CHUNKS = 2 * CTX_PASSES
QUAD = 4

HEAD_SHARE = 144
SHARES = (288, 192)

TURN_BANKS = 4
HISTORY_AHEAD = 4
WEIGHTS_AHEAD = 2
STORE_LAG = 4
W_RAW_BUFS = 8


def cols128(c):
    return slice(c * P, (c + 1) * P)


def tile_svdpp_context_gate_g1_kernel(
    tc, history, item_factors, context, w_context, b_context, user_factors, out_0, out_1, out_2
):
    nc = tc.nc
    with ExitStack() as stack:
        keep = stack.enter_context(tc.tile_pool(name="keep", bufs=1))
        ring = stack.enter_context(tc.tile_pool(name="ring", bufs=2))
        psum = stack.enter_context(tc.psum_pool(name="psum", bufs=2))
        stack.enter_context(tc.manual_schedule())

        tiles = {}

        ident = keep.tile([P, P], F32, name="ident")
        make_identity(nc, ident[:])


        def load_bias():
            b_rows = keep.tile([BIAS_ROWS, P], BF16, name="b_rows")
            nc.sync.dma_start(out=b_rows[:], in_=b_context.rearrange("(c p) -> c p", p=P))
            tiles["b_rows"] = b_rows

        def turn_bias():
            b_wide = keep.tile([P, P], F32, name="b_wide")
            nc.gpsimd.memset(b_wide[:], 0.0)
            nc.vector.tensor_copy(out=b_wide[0:BIAS_ROWS, :], in_=tiles["b_rows"][:])
            bank = psum.tile([P, P], F32, name="turn", bufs=TURN_BANKS)
            nc.tensor.transpose(bank[:], b_wide[:], ident[:])
            b_cols = keep.tile([P, BIAS_ROWS], F32, name="b_cols")
            nc.vector.tensor_copy(out=b_cols[:], in_=bank[:, 0:BIAS_ROWS])
            tiles["b_cols"] = b_cols

        def spread_bias(j):
            bank = psum.tile([P, NG], F32, name="turn", bufs=TURN_BANKS)
            for c in range(NG // P):
                col = j * NG // P + c
                nc.tensor.transpose(
                    bank[:, cols128(c)], tiles["b_cols"][:, col : col + 1].to_broadcast([P, P]), ident[:]
                )
            tiles["bias_bank", j] = bank

        def drain_bias(j):
            bias = keep.tile([P, NG], F32, name="bias%d" % j)
            nc.scalar.copy(out=bias[:], in_=tiles["bias_bank", j][:])
            tiles["bias", j] = bias


        def load_context(q):
            raw = ring.tile([P, 2, D], BF16, name="ctx_raw", bufs=3)
            rows = context[q * 2 * P : (q + 1) * 2 * P, :]
            nc.sync.dma_start(out=raw[:], in_=rows.rearrange("(a p) k -> p a k", p=P))
            tiles["ctx_raw", q] = raw

        def load_history(i):
            raw = ring.tile([P, I], BF16, name="hist_raw", bufs=HISTORY_AHEAD)
            nc.sync.dma_start(out=raw[:], in_=history[cols128(i), :])
            tiles["hist_raw", i] = raw

        def load_weight(j, g):
            src, first = (w_context, g) if g < CTX_PASSES else (item_factors, g - CTX_PASSES)
            raw = ring.tile([P, PACK, NG], BF16, name="w_raw", bufs=W_RAW_BUFS)
            nc.sync.dma_start(
                out=raw[:],
                in_=src[first * K_PASS : (first + 1) * K_PASS, j * NG : (j + 1) * NG].rearrange(
                    "(p t) n -> p t n", t=PACK
                ),
            )
            tiles["w_raw", j, g] = raw

        def load_user(s):
            j, i = divmod(s, TILES)
            raw = ring.tile([P, 2, NG], BF16, name="user", bufs=4)
            nc.sync.dma_start(
                out=raw[:],
                in_=user_factors[i * P : (i + 2) * P, j * NG : (j + 1) * NG].rearrange("(a p) n -> p a n", p=P),
            )
            tiles["user", s // 2] = raw


        def turn_pairs(key, sources):
            bank = psum.tile([P, 2, 2, P], F32, name="turn", bufs=TURN_BANKS)
            for a in range(2):
                for u in range(2):
                    nc.tensor.transpose(bank[:, a, u, :], sources[a].bitcast(F32)[:, u : 2 * P : 2], ident[:])
            tiles[key] = bank

        def drain_pairs(bank, grouped, count):
            nc.scalar.copy(
                out=grouped.bitcast(F32).rearrange("p (a r u) -> p a r u", a=count, u=2),
                in_=bank[:].rearrange("p a u r -> p a r u"),
            )

        def turn_context(chunk):
            q, g = divmod(chunk, CTX_PASSES)
            raw = tiles["ctx_raw", q]
            turn_pairs(("ctx_bank", chunk), [raw[:, a, g * K_PASS : (g + 1) * K_PASS] for a in range(2)])

        def drain_context(chunk):
            grouped = ring.tile([P, 2 * K_PASS], BF16, name="ctx_grouped", bufs=3, align_bytes=64)
            drain_pairs(tiles["ctx_bank", chunk], grouped[:], 2)
            tiles["ctx_grouped", chunk] = grouped

        def quantize_context(chunk):
            codes = keep.tile([P, 2 * P], U32, name="ctx_codes%d" % chunk, align_bytes=64)
            scales = keep.tile([P, 2 * P], U8, name="ctx_scales%d" % chunk, align_bytes=64)
            nc.vector.quantize_mx(out=codes[:].bitcast(FP8X4), scales=scales[:], in_=tiles["ctx_grouped", chunk][:])
            tiles["ctx_mx", chunk] = (codes, scales)

        def turn_history(i, h):
            raw = tiles["hist_raw", i]
            turn_pairs(("hist_bank", i, h), [raw[:, g * K_PASS : (g + 1) * K_PASS] for g in (2 * h, 2 * h + 1)])

        def drain_history(i, h):
            if h == 0:
                tiles["hist_grouped", i] = ring.tile([P, I], BF16, name="hist_grouped", align_bytes=64)
            drain_pairs(tiles["hist_bank", i, h], tiles["hist_grouped", i][:, h * 2 * K_PASS : (h + 1) * 2 * K_PASS], 2)

        def quantize_history(i):
            codes = keep.tile([P, ITEM_PASSES * P], U32, name="hist_codes%d" % i, align_bytes=64)
            scales = keep.tile([P, ITEM_PASSES * P], U8, name="hist_scales%d" % i, align_bytes=64)
            nc.vector.quantize_mx(out=codes[:].bitcast(FP8X4), scales=scales[:], in_=tiles["hist_grouped", i][:])
            tiles["hist_mx", i] = (codes, scales)


        def interleave_weight(j, g, c0, split, c1):
            if c0 == 0:
                tiles["w_grouped", j, g] = ring.tile([P, NG, PACK], BF16, name="w_grouped", bufs=3, align_bytes=64)
            for copy, cols in ((nc.vector.tensor_copy, slice(c0, split)), (nc.scalar.copy, slice(split, c1))):
                copy(
                    out=tiles["w_grouped", j, g][:, cols, :].rearrange("p (run col) t -> p run t col", col=4),
                    in_=tiles["w_raw", j, g][:, :, cols].rearrange("p t (run col) -> p run t col", col=4),
                )

        def quantize_weight(j, g, c0, c1):
            if c0 == 0:
                codes = ring.tile([P, NG], U32, name="w_codes", bufs=2 * PASSES, align_bytes=64)
                scales = ring.tile([P, NG], U8, name="w_scales", bufs=2 * PASSES, align_bytes=64)
                tiles["w_mx", j, g] = (codes, scales)
            codes, scales = tiles["w_mx", j, g]
            nc.vector.quantize_mx(
                out=codes[:, c0:c1].bitcast(FP8X4),
                scales=scales[:, c0:c1],
                in_=tiles["w_grouped", j, g][:, c0:c1, :].rearrange("p n t -> p (n t)"),
            )


        def mx_product(name, s, passes):
            bank = psum.tile([P, NG], F32, name=name)
            for g, (activations, users, weights) in enumerate(passes):
                nc.tensor.matmul_mx(
                    out=bank[:],
                    lhsT=activations[0][:, users].bitcast(FP8X4),
                    lhsT_scale=activations[1][:, users],
                    rhs=weights[0][:].bitcast(FP8X4),
                    rhs_scale=weights[1][:],
                    start=(g == 0),
                    stop=(g == len(passes) - 1),
                )
            tiles[name, s] = bank

        def multiply_logits(s):
            j, i = divmod(s, TILES)
            q, a = divmod(i, 2)
            passes = [(tiles["ctx_mx", CTX_PASSES * q + g], cols128(a), tiles["w_mx", j, g]) for g in range(CTX_PASSES)]
            mx_product("logits", s, passes)

        def multiply_implicit(s):
            j, i = divmod(s, TILES)
            passes = [(tiles["hist_mx", i], cols128(g), tiles["w_mx", j, CTX_PASSES + g]) for g in range(ITEM_PASSES)]
            mx_product("implicit", s, passes)


        def add_bias(s):
            z = ring.tile([P, NG], F32, name="z")
            nc.vector.tensor_tensor(out=z[:], in0=tiles["logits", s][:], in1=tiles["bias", s // TILES][:], op=ADD)
            tiles["z", s] = z

        def sigmoid(s):
            gate = ring.tile([P, NG], F32, name="gate", bufs=3)
            nc.scalar.activation(out=gate[:], in_=tiles["z", s][:], func=SIGMOID)
            tiles["gate", s] = gate

        def add_user(s):
            total = ring.tile([P, NG], F32, name="total", bufs=3)
            nc.vector.tensor_tensor(
                out=total[:], in0=tiles["implicit", s][:], in1=tiles["user", s // 2][:, s % 2, :], op=ADD
            )
            tiles["total", s] = total

        def apply_gate(s):
            y = ring.tile([P, NG], F32, name="y", bufs=STORE_LAG + 2)
            nc.vector.tensor_tensor(out=y[:], in0=tiles["total", s][:], in1=tiles["gate", s][:], op=MULT)
            tiles["y", s] = y


        def round_y(s, copy):
            y_bf = ring.tile([P, NG], BF16, name="y_bf", bufs=QUAD + 2)
            copy(
                out=y_bf[:].rearrange("m (u p e) -> m u p e", u=2, e=2),
                in_=tiles["y", s][:].rearrange("m (p u e) -> m u p e", u=2, e=2),
            )
            tiles["y_bf", s] = y_bf

        def turn_y(s, count):
            bank = psum.tile([P, count, 2, P], F32, name="turn", bufs=TURN_BANKS)
            for a in range(count):
                pairs = tiles["y_bf", s + a][:].bitcast(F32)
                for u in range(2):
                    nc.tensor.transpose(bank[:, a, u, :], pairs[:, cols128(u)], ident[:])
            tiles["y_bank", s] = bank

        def drain_y(s, count):
            grouped = ring.tile([P, count * K_PASS], BF16, name="y_grouped", align_bytes=64)
            drain_pairs(tiles["y_bank", s], grouped[:], count)
            tiles["y_grouped", s] = grouped

        def quantize_y(s, count):
            j, i = divmod(s, TILES)
            if i == 0:
                codes = ring.tile([P, T], U32, name="y_codes", align_bytes=64)
                scales = ring.tile([P, T], U8, name="y_scales", align_bytes=64)
                tiles["y_mx", j] = (codes, scales)
            codes, scales = tiles["y_mx", j]
            users = slice(i * P, (i + count) * P)
            nc.vector.quantize_mx(
                out=codes[:, users].bitcast(FP8X4), scales=scales[:, users], in_=tiles["y_grouped", s][:]
            )


        def store_y(s):
            j, i = divmod(s, TILES)
            nc.sync.dma_start(out=out_0[cols128(i), j * NG : (j + 1) * NG], in_=tiles["y", s][:])

        def store_codes(j, i0, i1):
            users = slice(i0 * P, i1 * P)
            words = out_1[j].rearrange("p m t -> p (m t)").bitcast(I32)
            nc.sync.dma_start(out=words[:, users], in_=tiles["y_mx", j][0][:, users].bitcast(I32))

        def store_scales(j, queues):
            scales = tiles["y_mx", j][1]
            for quadrant in range(4):
                queues[quadrant % len(queues)].dma_start(
                    out=out_2[j, 4 * quadrant : 4 * quadrant + 4, :].bitcast(I32),
                    in_=scales[32 * quadrant : 32 * quadrant + 4, :].bitcast(I32),
                )

        load_weight(0, 0)
        load_weight(0, 1)
        load_bias()
        for g in range(2, PASSES):
            index, is_history = divmod(g - 2, 2)
            if is_history:
                load_history(index)
            else:
                load_context(index)
            load_weight(0, g)
        load_history(2)
        load_user(0)
        load_context(2)
        load_history(3)
        load_weight(1, 0)

        def prepare_head_weight(g):
            interleave_weight(0, g, 0, HEAD_SHARE, HALF)
            if g >= 1:
                quantize_weight(0, g - 1, HALF, NG)
            interleave_weight(0, g, HALF, HALF + HEAD_SHARE, NG)
            quantize_weight(0, g, 0, HALF)

        def turn_and_drain_context(q):
            for chunk in (2 * q, 2 * q + 1):
                turn_context(chunk)
                drain_context(chunk)

        prepare_head_weight(0)
        turn_bias()
        prepare_head_weight(1)
        spread_bias(0)
        drain_bias(0)
        turn_and_drain_context(0)
        prepare_head_weight(2)
        quantize_context(0)
        quantize_context(1)
        for h in range(2):
            turn_history(0, h)
            drain_history(0, h)
        multiply_logits(0)
        prepare_head_weight(3)
        quantize_history(0)
        turn_and_drain_context(1)
        prepare_head_weight(4)
        quantize_context(2)
        quantize_context(3)
        prepare_head_weight(5)
        quantize_weight(0, PASSES - 1, HALF, NG)
        for h in range(2):
            turn_history(1, h)

        def weight_pass(s):
            j, i = divmod(s, TILES)
            return (j + 1, i - 1) if j + 1 < GROUPS and 1 <= i <= PASSES else None

        last = STEPS - 1
        loaded = 1
        interleaved = 0
        for s in range(STEPS + 1):
            j, i = divmod(s, TILES)
            y_first = s - 2 * QUAD + s % QUAD if s >= 2 * QUAD and s % QUAD < 2 else None

            if s + 1 < TILES:
                for h in range(2):
                    drain_history(s + 1, h)
            if HEAD_CHUNKS <= s + HEAD_CHUNKS - 1 < CTX_CHUNKS:
                drain_context(s + HEAD_CHUNKS - 1)
            if y_first is not None:
                drain_y(y_first, 2)
            if i == TILES - 1 and j + 1 < GROUPS:
                drain_bias(j + 1)

            if s >= 2:
                apply_gate(s - 2)
            if s >= 1:
                add_user(s - 1)
            if s < STEPS:
                add_bias(s)
            if s >= 2:
                round_y(s - 2, nc.scalar.copy)
            if s < STEPS:
                sigmoid(s)

            if s < STEPS:
                multiply_implicit(s)
            if s + 1 < STEPS:
                multiply_logits(s + 1)
            if s >= 2 * QUAD - 1 and s % QUAD == QUAD - 1:
                turn_y(s - 2 * QUAD + 1, 2)
                turn_y(s - 2 * QUAD + 3, 2)
            if s == STEPS:
                turn_y(last - 3, 2)
            if i == TILES - 2 and j + 1 < GROUPS:
                spread_bias(j + 1)
            if s + 2 < TILES:
                for h in range(2):
                    turn_history(s + 2, h)
            if s + HEAD_CHUNKS < CTX_CHUNKS:
                turn_context(s + HEAD_CHUNKS)

            if s + HISTORY_AHEAD < TILES:
                load_history(s + HISTORY_AHEAD)
            if s == 0:
                load_context(TILES // 2 - 1)
            if s % 2 == 0 and s + 2 < STEPS:
                load_user(s + 2)
            if weight_pass(s):
                interleaved = interleaved + 1
            while loaded < min(interleaved + WEIGHTS_AHEAD, (GROUPS - 1) * PASSES):
                load_weight(1 + loaded // PASSES, loaded % PASSES)
                loaded = loaded + 1
            if s >= STORE_LAG:
                store_y(s - STORE_LAG)
            if s >= 3 * QUAD - 1 and s % QUAD == QUAD - 1:
                done_j, done_i = divmod(s - 3 * QUAD + 1, TILES)
                store_codes(done_j, done_i, done_i + QUAD)
                if done_i + QUAD == TILES:
                    store_scales(done_j, [nc.sync])

            if s + 1 < TILES:
                quantize_history(s + 1)
            if HEAD_CHUNKS <= s + HEAD_CHUNKS - 1 < CTX_CHUNKS:
                quantize_context(s + HEAD_CHUNKS - 1)
            if s >= 1 and weight_pass(s - 1):
                quantize_weight(*weight_pass(s - 1), 0, NG)
            if weight_pass(s):
                interleave_weight(*weight_pass(s), 0, SHARES[j], NG)
            if y_first is not None:
                quantize_y(y_first, 2)

        drain_y(last - 5, 2)
        apply_gate(last)
        quantize_y(last - 5, 2)
        drain_y(last - 3, 2)
        turn_y(last - 1, 1)
        round_y(last, nc.vector.tensor_copy)
        for s in range(STEPS + 1 - STORE_LAG, STEPS):
            store_y(s)
        store_codes(GROUPS - 1, 0, QUAD)
        drain_y(last - 1, 1)
        turn_y(last, 1)
        quantize_y(last - 3, 2)
        quantize_y(last - 1, 1)
        store_codes(GROUPS - 1, QUAD, TILES - 1)
        drain_y(last, 1)
        quantize_y(last, 1)
        store_codes(GROUPS - 1, TILES - 1, TILES)
        store_scales(GROUPS - 1, [nc.sync, nc.scalar])
